import numpy as np
import ml_dtypes


def mxq(x, axis, fmt="e4m3"):
    dtype, down = {"e4m3": (ml_dtypes.float8_e4m3fn, 7), "e5m2": (ml_dtypes.float8_e5m2, 14)}[fmt]
    v = np.moveaxis(np.asarray(x, np.float32).astype(ml_dtypes.bfloat16).astype(np.float64), axis, -1)
    blocks = v.reshape(v.shape[:-1] + (-1, 32))
    amax = np.abs(blocks).max(-1, keepdims=True)
    byte = np.maximum(np.where(amax > 0, np.frexp(amax)[1] - 1 + 127, 0) - down, 1)
    scale = np.exp2(byte - 127.0)
    codes = (blocks / scale).astype(np.float32).astype(dtype).astype(np.float64)
    return np.moveaxis((codes * scale).reshape(v.shape), -1, axis)


WIDE = False


def mx_kscale(k):
    if not WIDE:
        return np.ones(k)
    levels = np.array([10, -10, 5, -5, 0])
    if k % 512:
        return np.exp2(np.random.permutation(np.resize(levels, k // 32))).repeat(32)
    a = np.empty((k // 512, 16))
    for p in range(k // 512):
        a[p, :8] = np.random.permutation(np.resize(levels, 8))
        for g in range(8):
            far = levels[np.abs(levels - a[p, g]) >= 10]
            a[p, g + 8] = far[np.random.randint(len(far))]
    return np.exp2(a.ravel()).repeat(32)


def f64(x):
    return np.asarray(x).astype(np.float64)


def striped(idx):
    return np.tile(np.asarray(idx).reshape(-1, 16).T, (8, 1)).astype(np.uint16)


def unstriped(offs):
    return offs[:16].T.reshape(-1).astype(np.int64)


E2M1 = np.array([0.0, 0.5, 1.0, 1.5, 2.0, 3.0, 4.0, 6.0, -0.0, -0.5, -1.0, -1.5, -2.0, -3.0, -4.0, -6.0])


def pack_weight(w, fmt):
    k, n = w.shape
    w = f64(np.asarray(w, np.float32).astype(ml_dtypes.bfloat16)).reshape(k // 32, 32, n)
    amax = np.abs(w).max(1)
    if fmt == "e4m3":
        byte = np.frexp(amax)[1] - 1 + 127 - 7
    else:
        mant, ex = np.frexp(amax / 6.0)
        byte = np.where(mant > 0.5, ex, ex - 1) + 127
    byte = np.clip(np.where(amax > 0, byte, 1), 1, 254)
    scaled = (w * np.exp2(127.0 - byte)[:, None, :]).reshape(k, n).astype(np.float32)
    by_word = np.ascontiguousarray(scaled.reshape(k // 512, 128, 4, n).transpose(0, 1, 3, 2))
    if fmt == "e4m3":
        words = by_word.astype(ml_dtypes.float8_e4m3fn).view(np.uint8)
    else:
        c = by_word.astype(ml_dtypes.float4_e2m1fn).view(np.uint8) & 0xF
        words = (c[..., 0::2] | (c[..., 1::2] << 4)).reshape(k // 512, 128, 2 * n)
    return np.ascontiguousarray(words), np.ascontiguousarray(byte.astype(np.uint8).reshape(k // 512, 16, n))


def unpack_weight(words, scales, fmt):
    g, _, n = scales.shape
    words = np.ascontiguousarray(words).reshape(g, 128, n, -1)
    if fmt == "e4m3":
        vals = words.view(ml_dtypes.float8_e4m3fn).astype(np.float64)
    else:
        nib = np.empty((g, 128, n, 4), np.uint8)
        nib[..., 0::2] = words & 0xF
        nib[..., 1::2] = words >> 4
        vals = E2M1[nib]
    vals = vals * np.repeat(np.exp2(scales.astype(np.float64) - 127.0), 8, axis=1)[..., None]
    return vals.transpose(0, 1, 3, 2).reshape(g * 512, n)


D, T, G, U, I, Q = 512, 1024, 256, 1024, 1024, 128


def setup_inputs():
    n = np.random.standard_normal
    idx = np.random.permutation(T)[:G]
    idx2 = np.random.randint(0, U, I)
    fd = mx_kscale(D)
    emitp = pack_weight(n((D, T)) / fd[:, None], "e2m1")
    return {
        "obs": (n((D, Q)) * 1.0 / np.sqrt(D) * fd[:, None]).astype(np.float32),
        "emit_words": emitp[0],
        "emit_scales": emitp[1],
        "cum": (1.0 * n((Q, U))).astype(np.float32),
        "step": (0.5 * n((1, I))).astype(np.float32),
        "offs": striped(idx),
        "offs2": striped(idx2),
    }


def reference(obs, emit_words, emit_scales, cum, step, offs, offs2):
    idx = unstriped(offs)
    idx2 = unstriped(offs2)
    emitu = unpack_weight(emit_words, emit_scales, "e2m1")
    s = f64(cum)[:, idx2] + f64(step)
    best = s.reshape(Q, G, I // G).max(axis=2)
    obsq = mxq(f64(obs), 0, "e4m3")
    emitidxg = emitu[:, idx]
    a = obsq.T @ emitidxg
    y = best + a
    return y

@@ -1,0 +1,117 @@
+from contextlib import ExitStack
+
+import concourse.mybir as mybir
+from concourse.masks import make_identity
+
+D, T, G, U, I, Q = 512, 1024, 256, 1024, 1024, 128
+FLOPS = 2 * D * Q * G
+
+F32 = mybir.dt.float32
+BF16 = mybir.dt.bfloat16
+I32 = mybir.dt.int32
+U32 = mybir.dt.uint32
+U16 = mybir.dt.uint16
+U8 = mybir.dt.uint8
+FP8X4 = mybir.dt.float8_e4m3fn_x4
+FP4X4 = mybir.dt.float4_e2m1fn_x4
+ADD = mybir.AluOpType.add
+MAX = mybir.AluOpType.max
+
+P = 128
+PACK = 4
+FAN = I // G
+HALVES = 2
+HALF_I = I // HALVES
+HALF_G = G // HALVES
+
+
+def tile_attend_viterbistep_kernel(tc, obs, emit_words, emit_scales, cum, step, offs, offs2, out):
+    nc = tc.nc
+    with ExitStack() as ctx:
+        sb = ctx.enter_context(tc.tile_pool(name="sb", bufs=1))
+        psum = ctx.enter_context(tc.psum_pool(name="psum", bufs=1))
+
+        state_list = sb.tile([P, G // 16], U16, name="state_list")
+        pred_list = sb.tile([P, I // 16], U16, name="pred_list")
+        words = sb.tile([P, T], U16, name="words", align_bytes=64)
+        scales = sb.tile([P, T], U8, name="scales", align_bytes=64)
+        cum_sb = sb.tile([P, U], F32, name="cum_sb")
+        step_cols = sb.tile([P, HALVES, 8], F32, name="step_cols", tag="early", align_bytes=64)
+        obs_sb = sb.tile([P, PACK, Q], F32, name="obs_sb", tag="late")
+        ident = sb.tile([P, P], F32, name="ident")
+
+        nc.vector.memset(scales[:].bitcast(I32), 0)
+        make_identity(nc, ident[:])
+
+        nc.sync.dma_start(state_list[:], offs)
+        nc.scalar.dma_start(step_cols[:, :, 0:FAN], step.rearrange("o (h n r) -> (o n) h r", h=HALVES, r=FAN))
+        nc.sync.dma_start(words[:].bitcast(I32), emit_words[0].bitcast(I32))
+        for quad in range(4):
+            nc.scalar.dma_start(
+                scales[32 * quad : 32 * quad + 4, :].bitcast(I32),
+                emit_scales[0, 4 * quad : 4 * quad + 4, :].bitcast(I32),
+            )
+        nc.sync.dma_start(cum_sb[:], cum)
+        nc.sync.dma_start(pred_list[:], offs2)
+        nc.sync.dma_start(obs_sb[:], obs.rearrange("(p j) q -> p j q", j=PACK))
+
+        banks = []
+        for h in range(HALVES):
+            bank = psum.tile([P, FAN, P], F32, name="step_bank%d" % h, tag="bank%d" % h)
+            for r in range(FAN):
+                nc.tensor.transpose(bank[:, r, :], step_cols[:, h, r : r + 1].to_broadcast([P, P]), ident[:])
+            banks.append(bank[:].rearrange("p r n -> p n r"))
+        rows_a = sb.tile([P, HALF_G, FAN], F32, name="rows_a")
+        rows_b = sb.tile([P, HALF_G // 2, FAN], F32, name="rows_b")
+        nc.scalar.copy(rows_a[:], banks[0])
+        nc.scalar.copy(rows_b[:], banks[1][:, : HALF_G // 2, :])
+
+        obs_bf = sb.tile([P, Q, PACK], BF16, name="obs_bf", tag="early", align_bytes=64)
+        nc.scalar.copy(obs_bf[:], obs_sb[:].rearrange("p j q -> p q j"))
+
+        rows_c = sb.tile([P, HALF_G // 2, FAN], F32, name="rows_c", tag="late")
+        nc.scalar.copy(rows_c[:], banks[1][:, HALF_G // 2 :, :])
+
+        words_g = sb.tile([P, G], U16, name="words_g", align_bytes=64)
+        scales_g = sb.tile([P, G], U8, name="scales_g", align_bytes=64)
+        nc.vector.tensor_copy(words_g[:], words[:].indirect(state_list[:]))
+        nc.vector.tensor_copy(scales_g[:], scales[:].indirect(state_list[:]))
+
+        obs_codes = sb.tile([P, Q], U32, name="obs_codes", align_bytes=64)
+        obs_scales = sb.tile([P, Q], U8, name="obs_scales", align_bytes=64)
+        acc = psum.tile([P, G], F32, name="acc", tag="bank0")
+
+        cand = [sb.tile([P, HALF_I], F32, name="cand%d" % h) for h in range(HALVES)]
+
+        def gather(dst, first, rows):
+            count = dst.shape[1]
+            listed = pred_list[:, first // 16 : (first + count) // 16]
+            nc.vector.tensor_tensor(dst, cum_sb[:].indirect(listed), rows[:].rearrange("p n r -> p (n r)"), ADD)
+
+        gather(cand[0][:], 0, rows_a)
+        gather(cand[1][:, : HALF_I // 2], HALF_I, rows_b)
+        nc.vector.quantize_mx(
+            out=obs_codes[:].bitcast(FP8X4), scales=obs_scales[:], in_=obs_bf[:].rearrange("p q j -> p (q j)")
+        )
+        nc.tensor.matmul_mx(
+            out=acc[:],
+            lhsT=obs_codes[:].bitcast(FP8X4),
+            lhsT_scale=obs_scales[:],
+            rhs=words_g[:].bitcast(FP4X4),
+            rhs_scale=scales_g[:],
+            start=True,
+            stop=True,
+        )
+        gather(cand[1][:, HALF_I // 2 :], HALF_I + HALF_I // 2, rows_c)
+
+        pair = [sb.tile([P, HALF_I // 2], F32, name="pair%d" % h) for h in range(HALVES)]
+        best = [sb.tile([P, HALF_G], F32, name="best%d" % h) for h in range(HALVES)]
+        res = [sb.tile([P, HALF_G], F32, name="res%d" % h) for h in range(HALVES)]
+        for h in range(HALVES):
+            nc.vector.tensor_tensor(pair[h][:], cand[h][:, 0::2], cand[h][:, 1::2], MAX)
+        for h in range(HALVES):
+            nc.vector.tensor_tensor(best[h][:], pair[h][:, 0::2], pair[h][:, 1::2], MAX)
+        for h in range(HALVES):
+            nc.vector.tensor_tensor(res[h][:], best[h][:], acc[:, h * HALF_G : (h + 1) * HALF_G], ADD)
+            queue = nc.sync if h == 0 else nc.scalar
+            queue.dma_start(out[:, h * HALF_G : (h + 1) * HALF_G], res[h][:])

@@ -40,14 +40,15 @@ def tile_attend_viterbistep_kernel(tc, obs, emit_words, emit_scales, cum, step, 
         obs_sb = sb.tile([P, PACK, Q], F32, name="obs_sb", tag="late")
         ident = sb.tile([P, P], F32, name="ident")
 
-        nc.vector.memset(scales[:].bitcast(I32), 0)
+        nc.gpsimd.memset(scales[:].bitcast(I32), 0)
         make_identity(nc, ident[:])
 
         nc.sync.dma_start(state_list[:], offs)
         nc.scalar.dma_start(step_cols[:, :, 0:FAN], step.rearrange("o (h n r) -> (o n) h r", h=HALVES, r=FAN))
         nc.sync.dma_start(words[:].bitcast(I32), emit_words[0].bitcast(I32))
         for quad in range(4):
-            nc.scalar.dma_start(
+            queue = nc.sync if quad < 2 else nc.scalar
+            queue.dma_start(
                 scales[32 * quad : 32 * quad + 4, :].bitcast(I32),
                 emit_scales[0, 4 * quad : 4 * quad + 4, :].bitcast(I32),
             )
@@ -55,62 +56,56 @@ def tile_attend_viterbistep_kernel(tc, obs, emit_words, emit_scales, cum, step, 
         nc.sync.dma_start(pred_list[:], offs2)
         nc.sync.dma_start(obs_sb[:], obs.rearrange("(p j) q -> p j q", j=PACK))
 
-        banks = []
+        step_rows = []
         for h in range(HALVES):
             bank = psum.tile([P, FAN, P], F32, name="step_bank%d" % h, tag="bank%d" % h)
             for r in range(FAN):
                 nc.tensor.transpose(bank[:, r, :], step_cols[:, h, r : r + 1].to_broadcast([P, P]), ident[:])
-            banks.append(bank[:].rearrange("p r n -> p n r"))
-        rows_a = sb.tile([P, HALF_G, FAN], F32, name="rows_a")
-        rows_b = sb.tile([P, HALF_G // 2, FAN], F32, name="rows_b")
-        nc.scalar.copy(rows_a[:], banks[0])
-        nc.scalar.copy(rows_b[:], banks[1][:, : HALF_G // 2, :])
+            rows = sb.tile([P, HALF_G, FAN], F32, name="step_rows%d" % h)
+            nc.scalar.copy(rows[:], bank[:].rearrange("p r n -> p n r"))
+            step_rows.append(rows)
 
         obs_bf = sb.tile([P, Q, PACK], BF16, name="obs_bf", tag="early", align_bytes=64)
         nc.scalar.copy(obs_bf[:], obs_sb[:].rearrange("p j q -> p q j"))
 
-        rows_c = sb.tile([P, HALF_G // 2, FAN], F32, name="rows_c", tag="late")
-        nc.scalar.copy(rows_c[:], banks[1][:, HALF_G // 2 :, :])
-
         words_g = sb.tile([P, G], U16, name="words_g", align_bytes=64)
         scales_g = sb.tile([P, G], U8, name="scales_g", align_bytes=64)
-        nc.vector.tensor_copy(words_g[:], words[:].indirect(state_list[:]))
         nc.vector.tensor_copy(scales_g[:], scales[:].indirect(state_list[:]))
+        nc.vector.tensor_copy(words_g[:], words[:].indirect(state_list[:]))
 
         obs_codes = sb.tile([P, Q], U32, name="obs_codes", align_bytes=64)
         obs_scales = sb.tile([P, Q], U8, name="obs_scales", align_bytes=64)
         acc = psum.tile([P, G], F32, name="acc", tag="bank0")
 
-        cand = [sb.tile([P, HALF_I], F32, name="cand%d" % h) for h in range(HALVES)]
+        cand = []
+        for h in range(HALVES):
+            s = sb.tile([P, HALF_I], F32, name="cand%d" % h)
+            cols = slice(h * HALF_I // 16, (h + 1) * HALF_I // 16)
+            nc.vector.tensor_tensor(
+                s[:], cum_sb[:].indirect(pred_list[:, cols]), step_rows[h][:].rearrange("p n r -> p (n r)"), ADD
+            )
+            cand.append(s)
+            if h == 1:
+                nc.vector.quantize_mx(
+                    out=obs_codes[:].bitcast(FP8X4), scales=obs_scales[:], in_=obs_bf[:].rearrange("p q j -> p (q j)")
+                )
+                nc.tensor.matmul_mx(
+                    out=acc[:],
+                    lhsT=obs_codes[:].bitcast(FP8X4),
+                    lhsT_scale=obs_scales[:],
+                    rhs=words_g[:].bitcast(FP4X4),
+                    rhs_scale=scales_g[:],
+                    start=True,
+                    stop=True,
+                )
 
-        def gather(dst, first, rows):
-            count = dst.shape[1]
-            listed = pred_list[:, first // 16 : (first + count) // 16]
-            nc.vector.tensor_tensor(dst, cum_sb[:].indirect(listed), rows[:].rearrange("p n r -> p (n r)"), ADD)
-
-        gather(cand[0][:], 0, rows_a)
-        gather(cand[1][:, : HALF_I // 2], HALF_I, rows_b)
-        nc.vector.quantize_mx(
-            out=obs_codes[:].bitcast(FP8X4), scales=obs_scales[:], in_=obs_bf[:].rearrange("p q j -> p (q j)")
-        )
-        nc.tensor.matmul_mx(
-            out=acc[:],
-            lhsT=obs_codes[:].bitcast(FP8X4),
-            lhsT_scale=obs_scales[:],
-            rhs=words_g[:].bitcast(FP4X4),
-            rhs_scale=scales_g[:],
-            start=True,
-            stop=True,
-        )
-        gather(cand[1][:, HALF_I // 2 :], HALF_I + HALF_I // 2, rows_c)
-
-        pair = [sb.tile([P, HALF_I // 2], F32, name="pair%d" % h) for h in range(HALVES)]
+        pair = sb.tile([P, HALVES, HALF_I // 2], F32, name="pair", tag="late")
         best = [sb.tile([P, HALF_G], F32, name="best%d" % h) for h in range(HALVES)]
         res = [sb.tile([P, HALF_G], F32, name="res%d" % h) for h in range(HALVES)]
         for h in range(HALVES):
-            nc.vector.tensor_tensor(pair[h][:], cand[h][:, 0::2], cand[h][:, 1::2], MAX)
+            nc.vector.tensor_tensor(pair[:, h, :], cand[h][:, 0::2], cand[h][:, 1::2], MAX)
         for h in range(HALVES):
-            nc.vector.tensor_tensor(best[h][:], pair[h][:, 0::2], pair[h][:, 1::2], MAX)
+            nc.vector.tensor_tensor(best[h][:], pair[:, h, 0::2], pair[:, h, 1::2], MAX)
         for h in range(HALVES):
             nc.vector.tensor_tensor(res[h][:], best[h][:], acc[:, h * HALF_G : (h + 1) * HALF_G], ADD)
             queue = nc.sync if h == 0 else nc.scalar

@@ -40,7 +40,7 @@ def tile_attend_viterbistep_kernel(tc, obs, emit_words, emit_scales, cum, step, 
         obs_sb = sb.tile([P, PACK, Q], F32, name="obs_sb", tag="late")
         ident = sb.tile([P, P], F32, name="ident")
 
-        nc.gpsimd.memset(scales[:].bitcast(I32), 0)
+        nc.vector.memset(scales[:].bitcast(I32), 0)
         make_identity(nc, ident[:])
 
         nc.sync.dma_start(state_list[:], offs)
@@ -56,13 +56,17 @@ def tile_attend_viterbistep_kernel(tc, obs, emit_words, emit_scales, cum, step, 
         nc.sync.dma_start(pred_list[:], offs2)
         nc.sync.dma_start(obs_sb[:], obs.rearrange("(p j) q -> p j q", j=PACK))
 
-        step_rows = []
+        pieces = ((0, 0, HALF_G // 2), (0, HALF_G // 2, HALF_G), (1, 0, HALF_G))
+        banks = []
         for h in range(HALVES):
             bank = psum.tile([P, FAN, P], F32, name="step_bank%d" % h, tag="bank%d" % h)
             for r in range(FAN):
                 nc.tensor.transpose(bank[:, r, :], step_cols[:, h, r : r + 1].to_broadcast([P, P]), ident[:])
-            rows = sb.tile([P, HALF_G, FAN], F32, name="step_rows%d" % h)
-            nc.scalar.copy(rows[:], bank[:].rearrange("p r n -> p n r"))
+            banks.append(bank[:].rearrange("p r n -> p n r"))
+        step_rows = []
+        for k, (h, g0, g1) in enumerate(pieces):
+            rows = sb.tile([P, g1 - g0, FAN], F32, name="step_rows%d" % k)
+            nc.scalar.copy(rows[:], banks[h][:, g0:g1, :])
             step_rows.append(rows)
 
         obs_bf = sb.tile([P, Q, PACK], BF16, name="obs_bf", tag="early", align_bytes=64)
@@ -70,34 +74,32 @@ def tile_attend_viterbistep_kernel(tc, obs, emit_words, emit_scales, cum, step, 
 
         words_g = sb.tile([P, G], U16, name="words_g", align_bytes=64)
         scales_g = sb.tile([P, G], U8, name="scales_g", align_bytes=64)
-        nc.vector.tensor_copy(scales_g[:], scales[:].indirect(state_list[:]))
         nc.vector.tensor_copy(words_g[:], words[:].indirect(state_list[:]))
+        nc.vector.tensor_copy(scales_g[:], scales[:].indirect(state_list[:]))
 
         obs_codes = sb.tile([P, Q], U32, name="obs_codes", align_bytes=64)
         obs_scales = sb.tile([P, Q], U8, name="obs_scales", align_bytes=64)
         acc = psum.tile([P, G], F32, name="acc", tag="bank0")
 
-        cand = []
-        for h in range(HALVES):
-            s = sb.tile([P, HALF_I], F32, name="cand%d" % h)
-            cols = slice(h * HALF_I // 16, (h + 1) * HALF_I // 16)
+        cand = [sb.tile([P, HALF_I], F32, name="cand%d" % h) for h in range(HALVES)]
+        for rows, (h, g0, g1) in zip(step_rows, pieces):
+            i0, i1 = FAN * g0, FAN * g1
+            listed = pred_list[:, (h * HALF_I + i0) // 16 : (h * HALF_I + i1) // 16]
             nc.vector.tensor_tensor(
-                s[:], cum_sb[:].indirect(pred_list[:, cols]), step_rows[h][:].rearrange("p n r -> p (n r)"), ADD
+                cand[h][:, i0:i1], cum_sb[:].indirect(listed), rows[:].rearrange("p n r -> p (n r)"), ADD
             )
-            cand.append(s)
-            if h == 1:
-                nc.vector.quantize_mx(
-                    out=obs_codes[:].bitcast(FP8X4), scales=obs_scales[:], in_=obs_bf[:].rearrange("p q j -> p (q j)")
-                )
-                nc.tensor.matmul_mx(
-                    out=acc[:],
-                    lhsT=obs_codes[:].bitcast(FP8X4),
-                    lhsT_scale=obs_scales[:],
-                    rhs=words_g[:].bitcast(FP4X4),
-                    rhs_scale=scales_g[:],
-                    start=True,
-                    stop=True,
-                )
+        nc.vector.quantize_mx(
+            out=obs_codes[:].bitcast(FP8X4), scales=obs_scales[:], in_=obs_bf[:].rearrange("p q j -> p (q j)")
+        )
+        nc.tensor.matmul_mx(
+            out=acc[:],
+            lhsT=obs_codes[:].bitcast(FP8X4),
+            lhsT_scale=obs_scales[:],
+            rhs=words_g[:].bitcast(FP4X4),
+            rhs_scale=scales_g[:],
+            start=True,
+            stop=True,
+        )
 
         pair = sb.tile([P, HALVES, HALF_I // 2], F32, name="pair", tag="late")
         best = [sb.tile([P, HALF_G], F32, name="best%d" % h) for h in range(HALVES)]
@@ -108,5 +110,5 @@ def tile_attend_viterbistep_kernel(tc, obs, emit_words, emit_scales, cum, step, 
             nc.vector.tensor_tensor(best[h][:], pair[:, h, 0::2], pair[:, h, 1::2], MAX)
         for h in range(HALVES):
             nc.vector.tensor_tensor(res[h][:], best[h][:], acc[:, h * HALF_G : (h + 1) * HALF_G], ADD)
-            queue = nc.sync if h == 0 else nc.scalar
+            queue = nc.scalar if h == 0 else nc.sync
             queue.dma_start(out[:, h * HALF_G : (h + 1) * HALF_G], res[h][:])

@@ -44,29 +44,24 @@ def tile_attend_viterbistep_kernel(tc, obs, emit_words, emit_scales, cum, step, 
         make_identity(nc, ident[:])
 
         nc.sync.dma_start(state_list[:], offs)
-        nc.scalar.dma_start(step_cols[:, :, 0:FAN], step.rearrange("o (h n r) -> (o n) h r", h=HALVES, r=FAN))
-        nc.sync.dma_start(words[:].bitcast(I32), emit_words[0].bitcast(I32))
+        nc.scalar.dma_start(words[:].bitcast(I32), emit_words[0].bitcast(I32))
+        nc.sync.dma_start(step_cols[:, :, 0:FAN], step.rearrange("o (h n r) -> (o n) h r", h=HALVES, r=FAN))
+        nc.scalar.dma_start(cum_sb[:], cum)
         for quad in range(4):
-            queue = nc.sync if quad < 2 else nc.scalar
-            queue.dma_start(
+            nc.sync.dma_start(
                 scales[32 * quad : 32 * quad + 4, :].bitcast(I32),
                 emit_scales[0, 4 * quad : 4 * quad + 4, :].bitcast(I32),
             )
-        nc.sync.dma_start(cum_sb[:], cum)
         nc.sync.dma_start(pred_list[:], offs2)
         nc.sync.dma_start(obs_sb[:], obs.rearrange("(p j) q -> p j q", j=PACK))
 
-        pieces = ((0, 0, HALF_G // 2), (0, HALF_G // 2, HALF_G), (1, 0, HALF_G))
-        banks = []
+        step_rows = []
         for h in range(HALVES):
             bank = psum.tile([P, FAN, P], F32, name="step_bank%d" % h, tag="bank%d" % h)
             for r in range(FAN):
                 nc.tensor.transpose(bank[:, r, :], step_cols[:, h, r : r + 1].to_broadcast([P, P]), ident[:])
-            banks.append(bank[:].rearrange("p r n -> p n r"))
-        step_rows = []
-        for k, (h, g0, g1) in enumerate(pieces):
-            rows = sb.tile([P, g1 - g0, FAN], F32, name="step_rows%d" % k)
-            nc.scalar.copy(rows[:], banks[h][:, g0:g1, :])
+            rows = sb.tile([P, HALF_G, FAN], F32, name="step_rows%d" % h)
+            nc.scalar.copy(rows[:], bank[:].rearrange("p r n -> p n r"))
             step_rows.append(rows)
 
         obs_bf = sb.tile([P, Q, PACK], BF16, name="obs_bf", tag="early", align_bytes=64)
@@ -81,25 +76,27 @@ def tile_attend_viterbistep_kernel(tc, obs, emit_words, emit_scales, cum, step, 
         obs_scales = sb.tile([P, Q], U8, name="obs_scales", align_bytes=64)
         acc = psum.tile([P, G], F32, name="acc", tag="bank0")
 
-        cand = [sb.tile([P, HALF_I], F32, name="cand%d" % h) for h in range(HALVES)]
-        for rows, (h, g0, g1) in zip(step_rows, pieces):
-            i0, i1 = FAN * g0, FAN * g1
-            listed = pred_list[:, (h * HALF_I + i0) // 16 : (h * HALF_I + i1) // 16]
+        cand = []
+        for h in range(HALVES):
+            s = sb.tile([P, HALF_I], F32, name="cand%d" % h)
+            cols = slice(h * HALF_I // 16, (h + 1) * HALF_I // 16)
             nc.vector.tensor_tensor(
-                cand[h][:, i0:i1], cum_sb[:].indirect(listed), rows[:].rearrange("p n r -> p (n r)"), ADD
+                s[:], cum_sb[:].indirect(pred_list[:, cols]), step_rows[h][:].rearrange("p n r -> p (n r)"), ADD
             )
-        nc.vector.quantize_mx(
-            out=obs_codes[:].bitcast(FP8X4), scales=obs_scales[:], in_=obs_bf[:].rearrange("p q j -> p (q j)")
-        )
-        nc.tensor.matmul_mx(
-            out=acc[:],
-            lhsT=obs_codes[:].bitcast(FP8X4),
-            lhsT_scale=obs_scales[:],
-            rhs=words_g[:].bitcast(FP4X4),
-            rhs_scale=scales_g[:],
-            start=True,
-            stop=True,
-        )
+            cand.append(s)
+            if h == 1:
+                nc.vector.quantize_mx(
+                    out=obs_codes[:].bitcast(FP8X4), scales=obs_scales[:], in_=obs_bf[:].rearrange("p q j -> p (q j)")
+                )
+                nc.tensor.matmul_mx(
+                    out=acc[:],
+                    lhsT=obs_codes[:].bitcast(FP8X4),
+                    lhsT_scale=obs_scales[:],
+                    rhs=words_g[:].bitcast(FP4X4),
+                    rhs_scale=scales_g[:],
+                    start=True,
+                    stop=True,
+                )
 
         pair = sb.tile([P, HALVES, HALF_I // 2], F32, name="pair", tag="late")
         best = [sb.tile([P, HALF_G], F32, name="best%d" % h) for h in range(HALVES)]

@@ -19,10 +19,15 @@ MAX = mybir.AluOpType.max
 
 P = 128
 PACK = 4
+BLOCKS = D // 32
+QUADRANTS = 4
+QUAD_ROWS = BLOCKS // QUADRANTS
+LIST_COL = 16
 FAN = I // G
 HALVES = 2
 HALF_I = I // HALVES
 HALF_G = G // HALVES
+STEP_PITCH = 8
 
 
 def tile_attend_viterbistep_kernel(tc, obs, emit_words, emit_scales, cum, step, offs, offs2, out):
@@ -31,28 +36,26 @@ def tile_attend_viterbistep_kernel(tc, obs, emit_words, emit_scales, cum, step, 
         sb = ctx.enter_context(tc.tile_pool(name="sb", bufs=1))
         psum = ctx.enter_context(tc.psum_pool(name="psum", bufs=1))
 
-        state_list = sb.tile([P, G // 16], U16, name="state_list")
-        pred_list = sb.tile([P, I // 16], U16, name="pred_list")
+        state_list = sb.tile([P, G // LIST_COL], U16, name="state_list")
+        pred_list = sb.tile([P, I // LIST_COL], U16, name="pred_list")
         words = sb.tile([P, T], U16, name="words", align_bytes=64)
         scales = sb.tile([P, T], U8, name="scales", align_bytes=64)
         cum_sb = sb.tile([P, U], F32, name="cum_sb")
-        step_cols = sb.tile([P, HALVES, 8], F32, name="step_cols", tag="early", align_bytes=64)
-        obs_sb = sb.tile([P, PACK, Q], F32, name="obs_sb", tag="late")
+        step_cols = sb.tile([P, HALVES, STEP_PITCH], F32, name="step_cols", tag="step_then_obs", align_bytes=64)
+        obs_sb = sb.tile([P, PACK, Q], F32, name="obs_sb", tag="obs_then_pairs")
         ident = sb.tile([P, P], F32, name="ident")
 
         nc.vector.memset(scales[:].bitcast(I32), 0)
         make_identity(nc, ident[:])
+        emit_plane = sb.tile([P, G], U8, name="emit_plane", align_bytes=64)
+        nc.gpsimd.memset(emit_plane[:].bitcast(I32), 0)
 
         nc.sync.dma_start(state_list[:], offs)
-        nc.scalar.dma_start(words[:].bitcast(I32), emit_words[0].bitcast(I32))
-        nc.sync.dma_start(step_cols[:, :, 0:FAN], step.rearrange("o (h n r) -> (o n) h r", h=HALVES, r=FAN))
-        nc.scalar.dma_start(cum_sb[:], cum)
-        for quad in range(4):
-            nc.sync.dma_start(
-                scales[32 * quad : 32 * quad + 4, :].bitcast(I32),
-                emit_scales[0, 4 * quad : 4 * quad + 4, :].bitcast(I32),
-            )
+        nc.scalar.dma_start(step_cols[:, :, 0:FAN], step.rearrange("o (h n r) -> (o n) h r", h=HALVES, r=FAN))
+        nc.sync.dma_start(words[:].bitcast(I32), emit_words[0].bitcast(I32))
+        nc.sync.dma_start(scales[0:BLOCKS, :].bitcast(I32), emit_scales[0].bitcast(I32))
         nc.sync.dma_start(pred_list[:], offs2)
+        nc.sync.dma_start(cum_sb[:], cum)
         nc.sync.dma_start(obs_sb[:], obs.rearrange("(p j) q -> p j q", j=PACK))
 
         step_rows = []
@@ -64,48 +67,54 @@ def tile_attend_viterbistep_kernel(tc, obs, emit_words, emit_scales, cum, step, 
             nc.scalar.copy(rows[:], bank[:].rearrange("p r n -> p n r"))
             step_rows.append(rows)
 
-        obs_bf = sb.tile([P, Q, PACK], BF16, name="obs_bf", tag="early", align_bytes=64)
+        obs_bf = sb.tile([P, Q, PACK], BF16, name="obs_bf", tag="step_then_obs", align_bytes=64)
         nc.scalar.copy(obs_bf[:], obs_sb[:].rearrange("p j q -> p q j"))
 
         words_g = sb.tile([P, G], U16, name="words_g", align_bytes=64)
         scales_g = sb.tile([P, G], U8, name="scales_g", align_bytes=64)
-        nc.vector.tensor_copy(words_g[:], words[:].indirect(state_list[:]))
         nc.vector.tensor_copy(scales_g[:], scales[:].indirect(state_list[:]))
+        nc.vector.tensor_copy(words_g[:], words[:].indirect(state_list[:]))
+
+        for quad in range(QUADRANTS):
+            nc.sync.dma_start(
+                emit_plane[32 * quad : 32 * quad + QUAD_ROWS, :].bitcast(I32),
+                scales_g[QUAD_ROWS * quad : QUAD_ROWS * (quad + 1), :].bitcast(I32),
+            )
 
         obs_codes = sb.tile([P, Q], U32, name="obs_codes", align_bytes=64)
-        obs_scales = sb.tile([P, Q], U8, name="obs_scales", align_bytes=64)
-        acc = psum.tile([P, G], F32, name="acc", tag="bank0")
+        obs_plane = sb.tile([P, Q], U8, name="obs_plane", align_bytes=64)
+        emission = psum.tile([P, G], F32, name="emission", tag="bank0")
 
         cand = []
         for h in range(HALVES):
-            s = sb.tile([P, HALF_I], F32, name="cand%d" % h)
-            cols = slice(h * HALF_I // 16, (h + 1) * HALF_I // 16)
+            scores = sb.tile([P, HALF_I], F32, name="cand%d" % h)
+            listed = pred_list[:, h * HALF_I // LIST_COL : (h + 1) * HALF_I // LIST_COL]
             nc.vector.tensor_tensor(
-                s[:], cum_sb[:].indirect(pred_list[:, cols]), step_rows[h][:].rearrange("p n r -> p (n r)"), ADD
+                scores[:], cum_sb[:].indirect(listed), step_rows[h][:].rearrange("p n r -> p (n r)"), ADD
             )
-            cand.append(s)
-            if h == 1:
-                nc.vector.quantize_mx(
-                    out=obs_codes[:].bitcast(FP8X4), scales=obs_scales[:], in_=obs_bf[:].rearrange("p q j -> p (q j)")
-                )
-                nc.tensor.matmul_mx(
-                    out=acc[:],
-                    lhsT=obs_codes[:].bitcast(FP8X4),
-                    lhsT_scale=obs_scales[:],
-                    rhs=words_g[:].bitcast(FP4X4),
-                    rhs_scale=scales_g[:],
-                    start=True,
-                    stop=True,
-                )
+            cand.append(scores)
 
-        pair = sb.tile([P, HALVES, HALF_I // 2], F32, name="pair", tag="late")
+        nc.vector.quantize_mx(
+            out=obs_codes[:].bitcast(FP8X4), scales=obs_plane[:], in_=obs_bf[:].rearrange("p q j -> p (q j)")
+        )
+        nc.tensor.matmul_mx(
+            out=emission[:],
+            lhsT=obs_codes[:].bitcast(FP8X4),
+            lhsT_scale=obs_plane[:],
+            rhs=words_g[:].bitcast(FP4X4),
+            rhs_scale=emit_plane[:],
+            start=True,
+            stop=True,
+        )
+
+        pairs = sb.tile([P, HALVES, HALF_I // 2], F32, name="pairs", tag="obs_then_pairs")
         best = [sb.tile([P, HALF_G], F32, name="best%d" % h) for h in range(HALVES)]
-        res = [sb.tile([P, HALF_G], F32, name="res%d" % h) for h in range(HALVES)]
+        result = [sb.tile([P, HALF_G], F32, name="result%d" % h) for h in range(HALVES)]
         for h in range(HALVES):
-            nc.vector.tensor_tensor(pair[:, h, :], cand[h][:, 0::2], cand[h][:, 1::2], MAX)
+            nc.vector.tensor_tensor(pairs[:, h, :], cand[h][:, 0::2], cand[h][:, 1::2], MAX)
         for h in range(HALVES):
-            nc.vector.tensor_tensor(best[h][:], pair[:, h, 0::2], pair[:, h, 1::2], MAX)
-        for h in range(HALVES):
-            nc.vector.tensor_tensor(res[h][:], best[h][:], acc[:, h * HALF_G : (h + 1) * HALF_G], ADD)
-            queue = nc.scalar if h == 0 else nc.sync
-            queue.dma_start(out[:, h * HALF_G : (h + 1) * HALF_G], res[h][:])
+            nc.vector.tensor_tensor(best[h][:], pairs[:, h, 0::2], pairs[:, h, 1::2], MAX)
+        for h, queue in enumerate((nc.scalar, nc.sync)):
+            states = slice(h * HALF_G, (h + 1) * HALF_G)
+            nc.vector.tensor_tensor(result[h][:], best[h][:], emission[:, states], ADD)
+            queue.dma_start(out[:, states], result[h][:])

@@ -45,15 +45,15 @@ def tile_attend_viterbistep_kernel(tc, obs, emit_words, emit_scales, cum, step, 
         obs_sb = sb.tile([P, PACK, Q], F32, name="obs_sb", tag="obs_then_pairs")
         ident = sb.tile([P, P], F32, name="ident")
 
-        nc.vector.memset(scales[:].bitcast(I32), 0)
+        nc.vector.memset(scales[0 : P - BLOCKS, :].bitcast(I32), 0)
         make_identity(nc, ident[:])
         emit_plane = sb.tile([P, G], U8, name="emit_plane", align_bytes=64)
         nc.gpsimd.memset(emit_plane[:].bitcast(I32), 0)
 
         nc.sync.dma_start(state_list[:], offs)
         nc.scalar.dma_start(step_cols[:, :, 0:FAN], step.rearrange("o (h n r) -> (o n) h r", h=HALVES, r=FAN))
+        nc.scalar.dma_start(scales[P - BLOCKS : P, :].bitcast(I32), emit_scales[0].bitcast(I32))
         nc.sync.dma_start(words[:].bitcast(I32), emit_words[0].bitcast(I32))
-        nc.sync.dma_start(scales[0:BLOCKS, :].bitcast(I32), emit_scales[0].bitcast(I32))
         nc.sync.dma_start(pred_list[:], offs2)
         nc.sync.dma_start(cum_sb[:], cum)
         nc.sync.dma_start(obs_sb[:], obs.rearrange("(p j) q -> p j q", j=PACK))
@@ -78,7 +78,7 @@ def tile_attend_viterbistep_kernel(tc, obs, emit_words, emit_scales, cum, step, 
         for quad in range(QUADRANTS):
             nc.sync.dma_start(
                 emit_plane[32 * quad : 32 * quad + QUAD_ROWS, :].bitcast(I32),
-                scales_g[QUAD_ROWS * quad : QUAD_ROWS * (quad + 1), :].bitcast(I32),
+                scales_g[P - BLOCKS + QUAD_ROWS * quad : P - BLOCKS + QUAD_ROWS * (quad + 1), :].bitcast(I32),
             )
 
         obs_codes = sb.tile([P, Q], U32, name="obs_codes", align_bytes=64)
@@ -107,14 +107,20 @@ def tile_attend_viterbistep_kernel(tc, obs, emit_words, emit_scales, cum, step, 
             stop=True,
         )
 
-        pairs = sb.tile([P, HALVES, HALF_I // 2], F32, name="pairs", tag="obs_then_pairs")
-        best = [sb.tile([P, HALF_G], F32, name="best%d" % h) for h in range(HALVES)]
+        pairs = sb.tile([P, I // 2], F32, name="pairs", tag="obs_then_pairs")
+        best = sb.tile([P, G], F32, name="best")
         result = [sb.tile([P, HALF_G], F32, name="result%d" % h) for h in range(HALVES)]
-        for h in range(HALVES):
-            nc.vector.tensor_tensor(pairs[:, h, :], cand[h][:, 0::2], cand[h][:, 1::2], MAX)
-        for h in range(HALVES):
-            nc.vector.tensor_tensor(best[h][:], pairs[:, h, 0::2], pairs[:, h, 1::2], MAX)
+        runs = ((0, 128), (128, 192), (192, 256))
+        for lo, hi in runs:
+            h, first = divmod(lo, HALF_G)
+            quads = cand[h][:, FAN * first : FAN * (first + hi - lo)].rearrange("p (n a b) -> p n a b", a=2, b=2)
+            nc.vector.tensor_tensor(
+                pairs[:, 2 * lo : 2 * hi].rearrange("p (n b) -> p n b", b=2), quads[:, :, 0, :], quads[:, :, 1, :], MAX
+            )
+        for lo, hi in runs:
+            nc.vector.tensor_tensor(best[:, lo:hi], pairs[:, 2 * lo : 2 * hi : 2], pairs[:, 2 * lo + 1 : 2 * hi : 2], MAX)
+        for lo, hi in runs:
+            h, first = divmod(lo, HALF_G)
+            nc.vector.tensor_tensor(result[h][:, first : first + hi - lo], best[:, lo:hi], emission[:, lo:hi], ADD)
         for h, queue in enumerate((nc.scalar, nc.sync)):
-            states = slice(h * HALF_G, (h + 1) * HALF_G)
-            nc.vector.tensor_tensor(result[h][:], best[h][:], emission[:, states], ADD)
-            queue.dma_start(out[:, states], result[h][:])
+            queue.dma_start(out[:, h * HALF_G : (h + 1) * HALF_G], result[h][:])

@@ -107,7 +107,7 @@ def tile_attend_viterbistep_kernel(tc, obs, emit_words, emit_scales, cum, step, 
             stop=True,
         )
 
-        pairs = sb.tile([P, I // 2], F32, name="pairs", tag="obs_then_pairs")
+        pairs = sb.tile([P, 2, G], F32, name="pairs", tag="obs_then_pairs")
         best = sb.tile([P, G], F32, name="best")
         result = [sb.tile([P, HALF_G], F32, name="result%d" % h) for h in range(HALVES)]
         runs = ((0, 128), (128, 192), (192, 256))
@@ -115,10 +115,10 @@ def tile_attend_viterbistep_kernel(tc, obs, emit_words, emit_scales, cum, step, 
             h, first = divmod(lo, HALF_G)
             quads = cand[h][:, FAN * first : FAN * (first + hi - lo)].rearrange("p (n a b) -> p n a b", a=2, b=2)
             nc.vector.tensor_tensor(
-                pairs[:, 2 * lo : 2 * hi].rearrange("p (n b) -> p n b", b=2), quads[:, :, 0, :], quads[:, :, 1, :], MAX
+                pairs[:, :, lo:hi].rearrange("p b n -> p n b"), quads[:, :, 0, :], quads[:, :, 1, :], MAX
             )
         for lo, hi in runs:
-            nc.vector.tensor_tensor(best[:, lo:hi], pairs[:, 2 * lo : 2 * hi : 2], pairs[:, 2 * lo + 1 : 2 * hi : 2], MAX)
+            nc.vector.tensor_tensor(best[:, lo:hi], pairs[:, 0, lo:hi], pairs[:, 1, lo:hi], MAX)
         for lo, hi in runs:
             h, first = divmod(lo, HALF_G)
             nc.vector.tensor_tensor(result[h][:, first : first + hi - lo], best[:, lo:hi], emission[:, lo:hi], ADD)

@@ -30,10 +30,16 @@ HALF_G = G // HALVES
 STEP_PITCH = 8
 
 
+FUSED = 128
+EARLY = 192
+COPY = mybir.ActivationFunctionType.Copy
+
+
 def tile_attend_viterbistep_kernel(tc, obs, emit_words, emit_scales, cum, step, offs, offs2, out):
     nc = tc.nc
     with ExitStack() as ctx:
         sb = ctx.enter_context(tc.tile_pool(name="sb", bufs=1))
+        shared = ctx.enter_context(tc.tile_pool(name="shared", bufs=1))
         psum = ctx.enter_context(tc.psum_pool(name="psum", bufs=1))
 
         state_list = sb.tile([P, G // LIST_COL], U16, name="state_list")
@@ -41,13 +47,13 @@ def tile_attend_viterbistep_kernel(tc, obs, emit_words, emit_scales, cum, step, 
         words = sb.tile([P, T], U16, name="words", align_bytes=64)
         scales = sb.tile([P, T], U8, name="scales", align_bytes=64)
         cum_sb = sb.tile([P, U], F32, name="cum_sb")
-        step_cols = sb.tile([P, HALVES, STEP_PITCH], F32, name="step_cols", tag="step_then_obs", align_bytes=64)
-        obs_sb = sb.tile([P, PACK, Q], F32, name="obs_sb", tag="obs_then_pairs")
+        step_cols = shared.tile([P, HALVES, STEP_PITCH], F32, name="step_cols", offset=1024 - 32)
+        obs_sb = sb.tile([P, PACK, Q], F32, name="obs_sb", tag="obs_then_looked_up")
         ident = sb.tile([P, P], F32, name="ident")
+        emit_plane = sb.tile([P, G], U8, name="emit_plane", align_bytes=64)
 
         nc.vector.memset(scales[0 : P - BLOCKS, :].bitcast(I32), 0)
         make_identity(nc, ident[:])
-        emit_plane = sb.tile([P, G], U8, name="emit_plane", align_bytes=64)
         nc.gpsimd.memset(emit_plane[:].bitcast(I32), 0)
 
         nc.sync.dma_start(state_list[:], offs)
@@ -58,42 +64,54 @@ def tile_attend_viterbistep_kernel(tc, obs, emit_words, emit_scales, cum, step, 
         nc.sync.dma_start(cum_sb[:], cum)
         nc.sync.dma_start(obs_sb[:], obs.rearrange("(p j) q -> p j q", j=PACK))
 
-        step_rows = []
+        banks = []
         for h in range(HALVES):
-            bank = psum.tile([P, FAN, P], F32, name="step_bank%d" % h, tag="bank%d" % h)
+            bank = psum.tile([P, FAN, P], F32, name="step_bank%d" % h)
             for r in range(FAN):
                 nc.tensor.transpose(bank[:, r, :], step_cols[:, h, r : r + 1].to_broadcast([P, P]), ident[:])
-            rows = sb.tile([P, HALF_G, FAN], F32, name="step_rows%d" % h)
-            nc.scalar.copy(rows[:], bank[:].rearrange("p r n -> p n r"))
-            step_rows.append(rows)
+            banks.append(bank)
 
-        obs_bf = sb.tile([P, Q, PACK], BF16, name="obs_bf", tag="step_then_obs", align_bytes=64)
-        nc.scalar.copy(obs_bf[:], obs_sb[:].rearrange("p j q -> p q j"))
+        def step_rows(lo, hi):
+            h, first = divmod(lo, HALF_G)
+            return banks[h][:, :, first : first + hi - lo].rearrange("p r n -> p n r")
 
-        words_g = sb.tile([P, G], U16, name="words_g", align_bytes=64)
+        def listed(lo, hi):
+            return cum_sb[:].indirect(pred_list[:, lo * FAN // LIST_COL : hi * FAN // LIST_COL])
+
+        def flat(ap):
+            return ap.rearrange("p n r -> p (n r)")
+
         scales_g = sb.tile([P, G], U8, name="scales_g", align_bytes=64)
+        words_g = sb.tile([P, G], U16, name="words_g", align_bytes=64)
         nc.vector.tensor_copy(scales_g[:], scales[:].indirect(state_list[:]))
         nc.vector.tensor_copy(words_g[:], words[:].indirect(state_list[:]))
-
         for quad in range(QUADRANTS):
             nc.sync.dma_start(
                 emit_plane[32 * quad : 32 * quad + QUAD_ROWS, :].bitcast(I32),
                 scales_g[P - BLOCKS + QUAD_ROWS * quad : P - BLOCKS + QUAD_ROWS * (quad + 1), :].bitcast(I32),
             )
 
+        fused_rows = sb.tile([P, FUSED, FAN], F32, name="fused_rows")
+        nc.scalar.copy(fused_rows[:], step_rows(0, FUSED))
+        cand = sb.tile([P, G, FAN], F32, name="cand")
+        nc.vector.tensor_tensor(flat(cand[:, 0:FUSED, :]), listed(0, FUSED), flat(fused_rows[:]), ADD)
+
+        looked_early = shared.tile([P, EARLY - FUSED, FAN], F32, name="looked_early", offset=1024)
+        nc.scalar.activation(flat(looked_early[:]), listed(FUSED, EARLY), COPY)
+        obs_bf = shared.tile([P, Q, PACK], BF16, name="obs_bf", align_bytes=64, offset=0)
+        nc.scalar.copy(obs_bf[:], obs_sb[:].rearrange("p j q -> p q j"))
+        looked_late = sb.tile([P, G - EARLY, FAN], F32, name="looked_late", tag="obs_then_looked_up")
+        nc.scalar.activation(flat(looked_late[:]), listed(EARLY, G), COPY)
+
+        def add_step(lo, hi):
+            looked, first = (looked_early, FUSED) if lo < EARLY else (looked_late, EARLY)
+            nc.vector.tensor_tensor(cand[:, lo:hi, :], looked[:, lo - first : hi - first, :], step_rows(lo, hi), ADD)
+
+        add_step(HALF_G, EARLY)
+
         obs_codes = sb.tile([P, Q], U32, name="obs_codes", align_bytes=64)
         obs_plane = sb.tile([P, Q], U8, name="obs_plane", align_bytes=64)
-        emission = psum.tile([P, G], F32, name="emission", tag="bank0")
-
-        cand = []
-        for h in range(HALVES):
-            scores = sb.tile([P, HALF_I], F32, name="cand%d" % h)
-            listed = pred_list[:, h * HALF_I // LIST_COL : (h + 1) * HALF_I // LIST_COL]
-            nc.vector.tensor_tensor(
-                scores[:], cum_sb[:].indirect(listed), step_rows[h][:].rearrange("p n r -> p (n r)"), ADD
-            )
-            cand.append(scores)
-
+        emission = psum.tile([P, G], F32, name="emission")
         nc.vector.quantize_mx(
             out=obs_codes[:].bitcast(FP8X4), scales=obs_plane[:], in_=obs_bf[:].rearrange("p q j -> p (q j)")
         )
@@ -107,20 +125,37 @@ def tile_attend_viterbistep_kernel(tc, obs, emit_words, emit_scales, cum, step, 
             stop=True,
         )
 
-        pairs = sb.tile([P, 2, G], F32, name="pairs", tag="obs_then_pairs")
+        pairs = [
+            shared.tile([P, 2, HALF_G], F32, name="pairs0", offset=0),
+            sb.tile([P, 2, HALF_G], F32, name="pairs1"),
+        ]
         best = sb.tile([P, G], F32, name="best")
         result = [sb.tile([P, HALF_G], F32, name="result%d" % h) for h in range(HALVES)]
-        runs = ((0, 128), (128, 192), (192, 256))
-        for lo, hi in runs:
+
+        def first_round(lo, hi):
             h, first = divmod(lo, HALF_G)
-            quads = cand[h][:, FAN * first : FAN * (first + hi - lo)].rearrange("p (n a b) -> p n a b", a=2, b=2)
-            nc.vector.tensor_tensor(
-                pairs[:, :, lo:hi].rearrange("p b n -> p n b"), quads[:, :, 0, :], quads[:, :, 1, :], MAX
-            )
-        for lo, hi in runs:
-            nc.vector.tensor_tensor(best[:, lo:hi], pairs[:, 0, lo:hi], pairs[:, 1, lo:hi], MAX)
-        for lo, hi in runs:
+            quads = cand[:, lo:hi, :].rearrange("p n (a b) -> p n a b", a=2)
+            kept = pairs[h][:, :, first : first + hi - lo].rearrange("p b n -> p n b")
+            nc.vector.tensor_tensor(kept, quads[:, :, 0, :], quads[:, :, 1, :], MAX)
+
+        def second_round(lo, hi):
+            h, first = divmod(lo, HALF_G)
+            cols = slice(first, first + hi - lo)
+            nc.vector.tensor_tensor(best[:, lo:hi], pairs[h][:, 0, cols], pairs[h][:, 1, cols], MAX)
+
+        def add_emission(lo, hi):
             h, first = divmod(lo, HALF_G)
             nc.vector.tensor_tensor(result[h][:, first : first + hi - lo], best[:, lo:hi], emission[:, lo:hi], ADD)
-        for h, queue in enumerate((nc.scalar, nc.sync)):
+
+        first_round(0, HALF_G)
+        add_step(EARLY, G)
+        second_round(0, HALF_G)
+        first_round(HALF_G, EARLY)
+        first_round(EARLY, G)
+        add_emission(0, HALF_G)
+        second_round(HALF_G, EARLY)
+        second_round(EARLY, G)
+        add_emission(HALF_G, EARLY)
+        add_emission(EARLY, G)
+        for h, queue in enumerate((nc.sync, nc.scalar)):
             queue.dma_start(out[:, h * HALF_G : (h + 1) * HALF_G], result[h][:])

@@ -27,16 +27,16 @@ FAN = I // G
 HALVES = 2
 HALF_I = I // HALVES
 HALF_G = G // HALVES
-STEP_PITCH = 8
 
 
-FUSED = 128
-EARLY = 192
+FUSED = 64
+LAST = 208
 COPY = mybir.ActivationFunctionType.Copy
 
 
 def tile_attend_viterbistep_kernel(tc, obs, emit_words, emit_scales, cum, step, offs, offs2, out):
     nc = tc.nc
+    runs = ((FUSED, HALF_G), (HALF_G, LAST), (LAST, G))
     with ExitStack() as ctx:
         sb = ctx.enter_context(tc.tile_pool(name="sb", bufs=1))
         shared = ctx.enter_context(tc.tile_pool(name="shared", bufs=1))
@@ -47,8 +47,8 @@ def tile_attend_viterbistep_kernel(tc, obs, emit_words, emit_scales, cum, step, 
         words = sb.tile([P, T], U16, name="words", align_bytes=64)
         scales = sb.tile([P, T], U8, name="scales", align_bytes=64)
         cum_sb = sb.tile([P, U], F32, name="cum_sb")
-        step_cols = shared.tile([P, HALVES, STEP_PITCH], F32, name="step_cols", offset=1024 - 32)
-        obs_sb = sb.tile([P, PACK, Q], F32, name="obs_sb", tag="obs_then_looked_up")
+        step_cols = shared.tile([P, HALVES, (G - FUSED) * FAN // HALVES], F32, name="step_cols", offset=0)
+        obs_sb = sb.tile([P, PACK, Q], F32, name="obs_sb")
         ident = sb.tile([P, P], F32, name="ident")
         emit_plane = sb.tile([P, G], U8, name="emit_plane", align_bytes=64)
 
@@ -91,27 +91,49 @@ def tile_attend_viterbistep_kernel(tc, obs, emit_words, emit_scales, cum, step, 
                 scales_g[P - BLOCKS + QUAD_ROWS * quad : P - BLOCKS + QUAD_ROWS * (quad + 1), :].bitcast(I32),
             )
 
-        fused_rows = sb.tile([P, FUSED, FAN], F32, name="fused_rows")
-        nc.scalar.copy(fused_rows[:], step_rows(0, FUSED))
-        cand = sb.tile([P, G, FAN], F32, name="cand")
-        nc.vector.tensor_tensor(flat(cand[:, 0:FUSED, :]), listed(0, FUSED), flat(fused_rows[:]), ADD)
+        obs_bf = sb.tile([P, Q, PACK], BF16, name="obs_bf", align_bytes=64)
+        nc.gpsimd.tensor_scalar(obs_bf[:], obs_sb[:].rearrange("p j q -> p q j"), 1.0, 0.0, mybir.AluOpType.mult, ADD)
 
-        looked_early = shared.tile([P, EARLY - FUSED, FAN], F32, name="looked_early", offset=1024)
-        nc.scalar.activation(flat(looked_early[:]), listed(FUSED, EARLY), COPY)
-        obs_bf = shared.tile([P, Q, PACK], BF16, name="obs_bf", align_bytes=64, offset=0)
-        nc.scalar.copy(obs_bf[:], obs_sb[:].rearrange("p j q -> p q j"))
-        looked_late = sb.tile([P, G - EARLY, FAN], F32, name="looked_late", tag="obs_then_looked_up")
-        nc.scalar.activation(flat(looked_late[:]), listed(EARLY, G), COPY)
+        cand_low = sb.tile([P, HALF_G, FAN], F32, name="cand_low")
+        fused_rows = cand_low[:, HALF_G - FUSED :, :]
+        nc.scalar.copy(fused_rows, step_rows(0, FUSED))
+        nc.vector.tensor_tensor(flat(cand_low[:, 0:FUSED, :]), listed(0, FUSED), flat(fused_rows), ADD)
+        looked = {}
+        for lo, hi in runs:
+            looked[lo] = shared.tile([P, hi - lo, FAN], F32, name="looked%d" % lo, offset=(lo - FUSED) * FAN * 4)
+            nc.scalar.activation(flat(looked[lo][:]), listed(lo, hi), COPY)
+
+        best = sb.tile([P, G], F32, name="best")
+        result = [sb.tile([P, HALF_G], F32, name="result%d" % h) for h in range(HALVES)]
+        emission = psum.tile([P, G], F32, name="emission")
+
+        def cand(lo, hi):
+            return cand_low[:, lo:hi, :] if lo < HALF_G else cand_high[:, lo - HALF_G : hi - HALF_G, :]
 
         def add_step(lo, hi):
-            looked, first = (looked_early, FUSED) if lo < EARLY else (looked_late, EARLY)
-            nc.vector.tensor_tensor(cand[:, lo:hi, :], looked[:, lo - first : hi - first, :], step_rows(lo, hi), ADD)
+            nc.vector.tensor_tensor(cand(lo, hi), looked[lo][:], step_rows(lo, hi), ADD)
 
-        add_step(HALF_G, EARLY)
+        def best_of_four(lo, hi):
+            nc.vector.tensor_reduce(best[:, lo:hi], cand(lo, hi), mybir.AxisListType.X, MAX)
+
+        def first_round(lo, hi):
+            quads = cand(lo, hi).rearrange("p n (a b) -> p n a b", a=2)
+            kept = pairs[:, :, lo - FUSED : hi - FUSED].rearrange("p b n -> p n b")
+            nc.vector.tensor_tensor(kept, quads[:, :, 0, :], quads[:, :, 1, :], MAX)
+
+        def second_round(lo, hi):
+            cols = slice(lo - FUSED, hi - FUSED)
+            nc.vector.tensor_tensor(best[:, lo:hi], pairs[:, 0, cols], pairs[:, 1, cols], MAX)
+
+        def add_emission(lo, hi):
+            h, first = divmod(lo, HALF_G)
+            nc.vector.tensor_tensor(result[h][:, first : first + hi - lo], best[:, lo:hi], emission[:, lo:hi], ADD)
+
+        add_step(*runs[0])
+        best_of_four(0, FUSED)
 
         obs_codes = sb.tile([P, Q], U32, name="obs_codes", align_bytes=64)
-        obs_plane = sb.tile([P, Q], U8, name="obs_plane", align_bytes=64)
-        emission = psum.tile([P, G], F32, name="emission")
+        obs_plane = shared.tile([P, Q], U8, name="obs_plane", align_bytes=64, offset=0)
         nc.vector.quantize_mx(
             out=obs_codes[:].bitcast(FP8X4), scales=obs_plane[:], in_=obs_bf[:].rearrange("p q j -> p (q j)")
         )
@@ -125,37 +147,16 @@ def tile_attend_viterbistep_kernel(tc, obs, emit_words, emit_scales, cum, step, 
             stop=True,
         )
 
-        pairs = [
-            shared.tile([P, 2, HALF_G], F32, name="pairs0", offset=0),
-            sb.tile([P, 2, HALF_G], F32, name="pairs1"),
-        ]
-        best = sb.tile([P, G], F32, name="best")
-        result = [sb.tile([P, HALF_G], F32, name="result%d" % h) for h in range(HALVES)]
-
-        def first_round(lo, hi):
-            h, first = divmod(lo, HALF_G)
-            quads = cand[:, lo:hi, :].rearrange("p n (a b) -> p n a b", a=2)
-            kept = pairs[h][:, :, first : first + hi - lo].rearrange("p b n -> p n b")
-            nc.vector.tensor_tensor(kept, quads[:, :, 0, :], quads[:, :, 1, :], MAX)
-
-        def second_round(lo, hi):
-            h, first = divmod(lo, HALF_G)
-            cols = slice(first, first + hi - lo)
-            nc.vector.tensor_tensor(best[:, lo:hi], pairs[h][:, 0, cols], pairs[h][:, 1, cols], MAX)
-
-        def add_emission(lo, hi):
-            h, first = divmod(lo, HALF_G)
-            nc.vector.tensor_tensor(result[h][:, first : first + hi - lo], best[:, lo:hi], emission[:, lo:hi], ADD)
-
-        first_round(0, HALF_G)
-        add_step(EARLY, G)
-        second_round(0, HALF_G)
-        first_round(HALF_G, EARLY)
-        first_round(EARLY, G)
+        cand_high = sb.tile([P, HALF_G, FAN], F32, name="cand_high")
+        pairs = sb.tile([P, 2, LAST - FUSED], F32, name="pairs")
+        add_step(*runs[1])
+        first_round(*runs[0])
+        add_step(*runs[2])
+        first_round(*runs[1])
+        best_of_four(*runs[2])
+        second_round(FUSED, LAST)
+        add_emission(*runs[2])
         add_emission(0, HALF_G)
-        second_round(HALF_G, EARLY)
-        second_round(EARLY, G)
-        add_emission(HALF_G, EARLY)
-        add_emission(EARLY, G)
+        add_emission(*runs[1])
         for h, queue in enumerate((nc.sync, nc.scalar)):
             queue.dma_start(out[:, h * HALF_G : (h + 1) * HALF_G], result[h][:])

@@ -95,9 +95,9 @@ def tile_attend_viterbistep_kernel(tc, obs, emit_words, emit_scales, cum, step, 
         nc.gpsimd.tensor_scalar(obs_bf[:], obs_sb[:].rearrange("p j q -> p q j"), 1.0, 0.0, mybir.AluOpType.mult, ADD)
 
         cand_low = sb.tile([P, HALF_G, FAN], F32, name="cand_low")
-        fused_rows = cand_low[:, HALF_G - FUSED :, :]
-        nc.scalar.copy(fused_rows, step_rows(0, FUSED))
-        nc.vector.tensor_tensor(flat(cand_low[:, 0:FUSED, :]), listed(0, FUSED), flat(fused_rows), ADD)
+        fused_rows = sb.tile([P, FUSED, FAN], F32, name="fused_rows")
+        nc.scalar.copy(fused_rows[:], step_rows(0, FUSED))
+        nc.vector.tensor_tensor(flat(cand_low[:, 0:FUSED, :]), listed(0, FUSED), flat(fused_rows[:]), ADD)
         looked = {}
         for lo, hi in runs:
             looked[lo] = shared.tile([P, hi - lo, FAN], F32, name="looked%d" % lo, offset=(lo - FUSED) * FAN * 4)

@@ -29,14 +29,14 @@ HALF_I = I // HALVES
 HALF_G = G // HALVES
 
 
-FUSED = 64
-LAST = 208
+FUSED = 96
+MID = 192
 COPY = mybir.ActivationFunctionType.Copy
 
 
 def tile_attend_viterbistep_kernel(tc, obs, emit_words, emit_scales, cum, step, offs, offs2, out):
     nc = tc.nc
-    runs = ((FUSED, HALF_G), (HALF_G, LAST), (LAST, G))
+    runs = ((HALF_G, MID), (MID, G), (FUSED, HALF_G))
     with ExitStack() as ctx:
         sb = ctx.enter_context(tc.tile_pool(name="sb", bufs=1))
         shared = ctx.enter_context(tc.tile_pool(name="shared", bufs=1))
@@ -94,46 +94,42 @@ def tile_attend_viterbistep_kernel(tc, obs, emit_words, emit_scales, cum, step, 
         obs_bf = sb.tile([P, Q, PACK], BF16, name="obs_bf", align_bytes=64)
         nc.gpsimd.tensor_scalar(obs_bf[:], obs_sb[:].rearrange("p j q -> p q j"), 1.0, 0.0, mybir.AluOpType.mult, ADD)
 
-        cand_low = sb.tile([P, HALF_G, FAN], F32, name="cand_low")
+        cand = sb.tile([P, G, FAN], F32, name="cand")
         fused_rows = sb.tile([P, FUSED, FAN], F32, name="fused_rows")
         nc.scalar.copy(fused_rows[:], step_rows(0, FUSED))
-        nc.vector.tensor_tensor(flat(cand_low[:, 0:FUSED, :]), listed(0, FUSED), flat(fused_rows[:]), ADD)
+        nc.vector.tensor_tensor(flat(cand[:, 0:FUSED, :]), listed(0, FUSED), flat(fused_rows[:]), ADD)
         looked = {}
         for lo, hi in runs:
             looked[lo] = shared.tile([P, hi - lo, FAN], F32, name="looked%d" % lo, offset=(lo - FUSED) * FAN * 4)
             nc.scalar.activation(flat(looked[lo][:]), listed(lo, hi), COPY)
 
+        pairs = sb.tile([P, 2, G], F32, name="pairs")
         best = sb.tile([P, G], F32, name="best")
-        result = [sb.tile([P, HALF_G], F32, name="result%d" % h) for h in range(HALVES)]
+        result = sb.tile([P, G], F32, name="result")
         emission = psum.tile([P, G], F32, name="emission")
 
-        def cand(lo, hi):
-            return cand_low[:, lo:hi, :] if lo < HALF_G else cand_high[:, lo - HALF_G : hi - HALF_G, :]
-
         def add_step(lo, hi):
-            nc.vector.tensor_tensor(cand(lo, hi), looked[lo][:], step_rows(lo, hi), ADD)
+            nc.vector.tensor_tensor(cand[:, lo:hi, :], looked[lo][:], step_rows(lo, hi), ADD)
 
         def best_of_four(lo, hi):
-            nc.vector.tensor_reduce(best[:, lo:hi], cand(lo, hi), mybir.AxisListType.X, MAX)
+            nc.vector.tensor_reduce(best[:, lo:hi], cand[:, lo:hi, :], mybir.AxisListType.X, MAX)
 
         def first_round(lo, hi):
-            quads = cand(lo, hi).rearrange("p n (a b) -> p n a b", a=2)
-            kept = pairs[:, :, lo - FUSED : hi - FUSED].rearrange("p b n -> p n b")
+            quads = cand[:, lo:hi, :].rearrange("p n (a b) -> p n a b", a=2)
+            kept = pairs[:, :, lo:hi].rearrange("p b n -> p n b")
             nc.vector.tensor_tensor(kept, quads[:, :, 0, :], quads[:, :, 1, :], MAX)
 
         def second_round(lo, hi):
-            cols = slice(lo - FUSED, hi - FUSED)
-            nc.vector.tensor_tensor(best[:, lo:hi], pairs[:, 0, cols], pairs[:, 1, cols], MAX)
+            nc.vector.tensor_tensor(best[:, lo:hi], pairs[:, 0, lo:hi], pairs[:, 1, lo:hi], MAX)
 
         def add_emission(lo, hi):
-            h, first = divmod(lo, HALF_G)
-            nc.vector.tensor_tensor(result[h][:, first : first + hi - lo], best[:, lo:hi], emission[:, lo:hi], ADD)
+            nc.vector.tensor_tensor(result[:, lo:hi], best[:, lo:hi], emission[:, lo:hi], ADD)
 
         add_step(*runs[0])
-        best_of_four(0, FUSED)
+        first_round(0, FUSED)
 
         obs_codes = sb.tile([P, Q], U32, name="obs_codes", align_bytes=64)
-        obs_plane = shared.tile([P, Q], U8, name="obs_plane", align_bytes=64, offset=0)
+        obs_plane = shared.tile([P, Q], U8, name="obs_plane", align_bytes=64, offset=(HALF_G - FUSED) * FAN * 4)
         nc.vector.quantize_mx(
             out=obs_codes[:].bitcast(FP8X4), scales=obs_plane[:], in_=obs_bf[:].rearrange("p q j -> p (q j)")
         )
@@ -147,16 +143,14 @@ def tile_attend_viterbistep_kernel(tc, obs, emit_words, emit_scales, cum, step, 
             stop=True,
         )
 
-        cand_high = sb.tile([P, HALF_G, FAN], F32, name="cand_high")
-        pairs = sb.tile([P, 2, LAST - FUSED], F32, name="pairs")
-        add_step(*runs[1])
         first_round(*runs[0])
+        add_step(*runs[1])
+        second_round(0, FUSED)
         add_step(*runs[2])
         first_round(*runs[1])
         best_of_four(*runs[2])
-        second_round(FUSED, LAST)
-        add_emission(*runs[2])
+        second_round(HALF_G, G)
         add_emission(0, HALF_G)
-        add_emission(*runs[1])
+        add_emission(HALF_G, G)
         for h, queue in enumerate((nc.sync, nc.scalar)):
-            queue.dma_start(out[:, h * HALF_G : (h + 1) * HALF_G], result[h][:])
+            queue.dma_start(out[:, h * HALF_G : (h + 1) * HALF_G], result[:, h * HALF_G : (h + 1) * HALF_G])

@@ -126,7 +126,7 @@ def tile_attend_viterbistep_kernel(tc, obs, emit_words, emit_scales, cum, step, 
             nc.vector.tensor_tensor(result[:, lo:hi], best[:, lo:hi], emission[:, lo:hi], ADD)
 
         add_step(*runs[0])
-        first_round(0, FUSED)
+        best_of_four(0, FUSED)
 
         obs_codes = sb.tile([P, Q], U32, name="obs_codes", align_bytes=64)
         obs_plane = shared.tile([P, Q], U8, name="obs_plane", align_bytes=64, offset=(HALF_G - FUSED) * FAN * 4)
@@ -143,9 +143,8 @@ def tile_attend_viterbistep_kernel(tc, obs, emit_words, emit_scales, cum, step, 
             stop=True,
         )
 
-        first_round(*runs[0])
         add_step(*runs[1])
-        second_round(0, FUSED)
+        first_round(*runs[0])
         add_step(*runs[2])
         first_round(*runs[1])
         best_of_four(*runs[2])

@@ -127,6 +127,7 @@ def tile_attend_viterbistep_kernel(tc, obs, emit_words, emit_scales, cum, step, 
 
         add_step(*runs[0])
         best_of_four(0, FUSED)
+        add_step(*runs[1])
 
         obs_codes = sb.tile([P, Q], U32, name="obs_codes", align_bytes=64)
         obs_plane = shared.tile([P, Q], U8, name="obs_plane", align_bytes=64, offset=(HALF_G - FUSED) * FAN * 4)
@@ -143,7 +144,6 @@ def tile_attend_viterbistep_kernel(tc, obs, emit_words, emit_scales, cum, step, 
             stop=True,
         )
 
-        add_step(*runs[1])
         first_round(*runs[0])
         add_step(*runs[2])
         first_round(*runs[1])

@@ -126,7 +126,7 @@ def tile_attend_viterbistep_kernel(tc, obs, emit_words, emit_scales, cum, step, 
             nc.vector.tensor_tensor(result[:, lo:hi], best[:, lo:hi], emission[:, lo:hi], ADD)
 
         add_step(*runs[0])
-        best_of_four(0, FUSED)
+        best_of_four(0, HALF_G // 2)
         add_step(*runs[1])
 
         obs_codes = sb.tile([P, Q], U32, name="obs_codes", align_bytes=64)
@@ -144,10 +144,9 @@ def tile_attend_viterbistep_kernel(tc, obs, emit_words, emit_scales, cum, step, 
             stop=True,
         )
 
-        first_round(*runs[0])
         add_step(*runs[2])
-        first_round(*runs[1])
-        best_of_four(*runs[2])
+        first_round(HALF_G, G)
+        best_of_four(HALF_G // 2, HALF_G)
         second_round(HALF_G, G)
         add_emission(0, HALF_G)
         add_emission(HALF_G, G)

@@ -56,10 +56,10 @@ def tile_attend_viterbistep_kernel(tc, obs, emit_words, emit_scales, cum, step, 
         make_identity(nc, ident[:])
         nc.gpsimd.memset(emit_plane[:].bitcast(I32), 0)
 
-        nc.sync.dma_start(state_list[:], offs)
-        nc.scalar.dma_start(step_cols[:, :, 0:FAN], step.rearrange("o (h n r) -> (o n) h r", h=HALVES, r=FAN))
+        nc.sync.dma_start(step_cols[:, :, 0:FAN], step.rearrange("o (h n r) -> (o n) h r", h=HALVES, r=FAN))
         nc.scalar.dma_start(scales[P - BLOCKS : P, :].bitcast(I32), emit_scales[0].bitcast(I32))
-        nc.sync.dma_start(words[:].bitcast(I32), emit_words[0].bitcast(I32))
+        nc.sync.dma_start(state_list[:], offs)
+        nc.scalar.dma_start(words[:].bitcast(I32), emit_words[0].bitcast(I32))
         nc.sync.dma_start(pred_list[:], offs2)
         nc.sync.dma_start(cum_sb[:], cum)
         nc.sync.dma_start(obs_sb[:], obs.rearrange("(p j) q -> p j q", j=PACK))
@@ -150,5 +150,5 @@ def tile_attend_viterbistep_kernel(tc, obs, emit_words, emit_scales, cum, step, 
         second_round(HALF_G, G)
         add_emission(0, HALF_G)
         add_emission(HALF_G, G)
-        for h, queue in enumerate((nc.sync, nc.scalar)):
+        for h, queue in enumerate((nc.scalar, nc.sync)):
             queue.dma_start(out[:, h * HALF_G : (h + 1) * HALF_G], result[:, h * HALF_G : (h + 1) * HALF_G])

@@ -29,14 +29,15 @@ HALF_I = I // HALVES
 HALF_G = G // HALVES
 
 
-FUSED = 96
+OWN = 56
 MID = 192
+EARLY = 64
 COPY = mybir.ActivationFunctionType.Copy
+ROW = FAN * 4
 
 
 def tile_attend_viterbistep_kernel(tc, obs, emit_words, emit_scales, cum, step, offs, offs2, out):
     nc = tc.nc
-    runs = ((HALF_G, MID), (MID, G), (FUSED, HALF_G))
     with ExitStack() as ctx:
         sb = ctx.enter_context(tc.tile_pool(name="sb", bufs=1))
         shared = ctx.enter_context(tc.tile_pool(name="shared", bufs=1))
@@ -47,7 +48,7 @@ def tile_attend_viterbistep_kernel(tc, obs, emit_words, emit_scales, cum, step, 
         words = sb.tile([P, T], U16, name="words", align_bytes=64)
         scales = sb.tile([P, T], U8, name="scales", align_bytes=64)
         cum_sb = sb.tile([P, U], F32, name="cum_sb")
-        step_cols = shared.tile([P, HALVES, (G - FUSED) * FAN // HALVES], F32, name="step_cols", offset=0)
+        step_cols = sb.tile([P, HALVES, FAN], F32, name="step_cols")
         obs_sb = sb.tile([P, PACK, Q], F32, name="obs_sb")
         ident = sb.tile([P, P], F32, name="ident")
         emit_plane = sb.tile([P, G], U8, name="emit_plane", align_bytes=64)
@@ -56,13 +57,17 @@ def tile_attend_viterbistep_kernel(tc, obs, emit_words, emit_scales, cum, step, 
         make_identity(nc, ident[:])
         nc.gpsimd.memset(emit_plane[:].bitcast(I32), 0)
 
-        nc.sync.dma_start(step_cols[:, :, 0:FAN], step.rearrange("o (h n r) -> (o n) h r", h=HALVES, r=FAN))
+        nc.sync.dma_start(step_cols[:], step.rearrange("o (h n r) -> (o n) h r", h=HALVES, r=FAN))
         nc.scalar.dma_start(scales[P - BLOCKS : P, :].bitcast(I32), emit_scales[0].bitcast(I32))
         nc.sync.dma_start(state_list[:], offs)
-        nc.scalar.dma_start(words[:].bitcast(I32), emit_words[0].bitcast(I32))
+        nc.scalar.dma_start(cum_sb[:], cum)
         nc.sync.dma_start(pred_list[:], offs2)
-        nc.sync.dma_start(cum_sb[:], cum)
+        nc.sync.dma_start(words[:].bitcast(I32), emit_words[0].bitcast(I32))
         nc.sync.dma_start(obs_sb[:], obs.rearrange("(p j) q -> p j q", j=PACK))
+
+        warm = sb.tile([P, 16], F32, name="warm")
+        nc.vector.memset(warm[:, 0:1], 0.0)
+        nc.scalar.activation(warm[:, 8:9], warm[:, 0:1], COPY)
 
         banks = []
         for h in range(HALVES):
@@ -82,55 +87,48 @@ def tile_attend_viterbistep_kernel(tc, obs, emit_words, emit_scales, cum, step, 
             return ap.rearrange("p n r -> p (n r)")
 
         scales_g = sb.tile([P, G], U8, name="scales_g", align_bytes=64)
-        words_g = sb.tile([P, G], U16, name="words_g", align_bytes=64)
         nc.vector.tensor_copy(scales_g[:], scales[:].indirect(state_list[:]))
-        nc.vector.tensor_copy(words_g[:], words[:].indirect(state_list[:]))
         for quad in range(QUADRANTS):
             nc.sync.dma_start(
                 emit_plane[32 * quad : 32 * quad + QUAD_ROWS, :].bitcast(I32),
                 scales_g[P - BLOCKS + QUAD_ROWS * quad : P - BLOCKS + QUAD_ROWS * (quad + 1), :].bitcast(I32),
             )
 
+        looked_lo = sb.tile([P, HALF_G, FAN], F32, name="looked_lo")
+        looked_mid = shared.tile([P, MID - HALF_G, FAN], F32, name="looked_mid", offset=0)
+        looked_last = sb.tile([P, G - MID, FAN], F32, name="looked_last")
+        nc.vector.tensor_copy(flat(looked_lo[:, 0:OWN, :]), listed(0, OWN))
+        nc.scalar.activation(flat(looked_lo[:, OWN:HALF_G, :]), listed(OWN, HALF_G), COPY)
+        nc.scalar.activation(flat(looked_mid[:]), listed(HALF_G, MID), COPY)
+        nc.scalar.activation(flat(looked_last[:]), listed(MID, G), COPY)
+
+        words_g = sb.tile([P, G], U16, name="words_g", align_bytes=64)
+        nc.vector.tensor_copy(words_g[:], words[:].indirect(state_list[:]))
+
         obs_bf = sb.tile([P, Q, PACK], BF16, name="obs_bf", align_bytes=64)
         nc.gpsimd.tensor_scalar(obs_bf[:], obs_sb[:].rearrange("p j q -> p q j"), 1.0, 0.0, mybir.AluOpType.mult, ADD)
 
-        cand = sb.tile([P, G, FAN], F32, name="cand")
-        fused_rows = sb.tile([P, FUSED, FAN], F32, name="fused_rows")
-        nc.scalar.copy(fused_rows[:], step_rows(0, FUSED))
-        nc.vector.tensor_tensor(flat(cand[:, 0:FUSED, :]), listed(0, FUSED), flat(fused_rows[:]), ADD)
-        looked = {}
-        for lo, hi in runs:
-            looked[lo] = shared.tile([P, hi - lo, FAN], F32, name="looked%d" % lo, offset=(lo - FUSED) * FAN * 4)
-            nc.scalar.activation(flat(looked[lo][:]), listed(lo, hi), COPY)
-
-        pairs = sb.tile([P, 2, G], F32, name="pairs")
+        cand = sb.tile([P, MID, FAN], F32, name="cand")
+        pairs = sb.tile([P, 2, MID], F32, name="pairs")
         best = sb.tile([P, G], F32, name="best")
         result = sb.tile([P, G], F32, name="result")
         emission = psum.tile([P, G], F32, name="emission")
-
-        def add_step(lo, hi):
-            nc.vector.tensor_tensor(cand[:, lo:hi, :], looked[lo][:], step_rows(lo, hi), ADD)
-
-        def best_of_four(lo, hi):
-            nc.vector.tensor_reduce(best[:, lo:hi], cand[:, lo:hi, :], mybir.AxisListType.X, MAX)
 
         def first_round(lo, hi):
             quads = cand[:, lo:hi, :].rearrange("p n (a b) -> p n a b", a=2)
             kept = pairs[:, :, lo:hi].rearrange("p b n -> p n b")
             nc.vector.tensor_tensor(kept, quads[:, :, 0, :], quads[:, :, 1, :], MAX)
 
-        def second_round(lo, hi):
-            nc.vector.tensor_tensor(best[:, lo:hi], pairs[:, 0, lo:hi], pairs[:, 1, lo:hi], MAX)
-
-        def add_emission(lo, hi):
+        def finish(lo, hi, queue):
             nc.vector.tensor_tensor(result[:, lo:hi], best[:, lo:hi], emission[:, lo:hi], ADD)
+            queue.dma_start(out[:, lo:hi], result[:, lo:hi])
 
-        add_step(*runs[0])
-        best_of_four(0, HALF_G // 2)
-        add_step(*runs[1])
+        nc.vector.tensor_tensor(cand[:, 0:HALF_G, :], looked_lo[:], step_rows(0, HALF_G), ADD)
+        nc.vector.tensor_tensor(cand[:, HALF_G:MID, :], looked_mid[:], step_rows(HALF_G, MID), ADD)
+        nc.vector.tensor_reduce(best[:, 0:EARLY], cand[:, 0:EARLY, :], mybir.AxisListType.X, MAX)
 
         obs_codes = sb.tile([P, Q], U32, name="obs_codes", align_bytes=64)
-        obs_plane = shared.tile([P, Q], U8, name="obs_plane", align_bytes=64, offset=(HALF_G - FUSED) * FAN * 4)
+        obs_plane = shared.tile([P, Q], U8, name="obs_plane", align_bytes=64, offset=0)
         nc.vector.quantize_mx(
             out=obs_codes[:].bitcast(FP8X4), scales=obs_plane[:], in_=obs_bf[:].rearrange("p q j -> p (q j)")
         )
@@ -144,11 +142,10 @@ def tile_attend_viterbistep_kernel(tc, obs, emit_words, emit_scales, cum, step, 
             stop=True,
         )
 
-        add_step(*runs[2])
-        first_round(HALF_G, G)
-        best_of_four(HALF_G // 2, HALF_G)
-        second_round(HALF_G, G)
-        add_emission(0, HALF_G)
-        add_emission(HALF_G, G)
-        for h, queue in enumerate((nc.scalar, nc.sync)):
-            queue.dma_start(out[:, h * HALF_G : (h + 1) * HALF_G], result[:, h * HALF_G : (h + 1) * HALF_G])
+        cand_last = shared.tile([P, G - MID, FAN], F32, name="cand_last", offset=Q)
+        first_round(EARLY, MID)
+        nc.vector.tensor_tensor(cand_last[:], looked_last[:], step_rows(MID, G), ADD)
+        nc.vector.tensor_tensor(best[:, EARLY:MID], pairs[:, 0, EARLY:MID], pairs[:, 1, EARLY:MID], MAX)
+        nc.vector.tensor_reduce(best[:, MID:G], cand_last[:], mybir.AxisListType.X, MAX)
+        finish(0, MID, nc.scalar)
+        finish(MID, G, nc.sync)

@@ -31,7 +31,6 @@ HALF_G = G // HALVES
 
 OWN = 56
 MID = 192
-EARLY = 64
 COPY = mybir.ActivationFunctionType.Copy
 ROW = FAN * 4
 
@@ -94,8 +93,8 @@ def tile_attend_viterbistep_kernel(tc, obs, emit_words, emit_scales, cum, step, 
                 scales_g[P - BLOCKS + QUAD_ROWS * quad : P - BLOCKS + QUAD_ROWS * (quad + 1), :].bitcast(I32),
             )
 
-        looked_lo = sb.tile([P, HALF_G, FAN], F32, name="looked_lo")
-        looked_mid = shared.tile([P, MID - HALF_G, FAN], F32, name="looked_mid", offset=0)
+        looked_lo = shared.tile([P, HALF_G, FAN], F32, name="looked_lo", offset=0)
+        looked_mid = sb.tile([P, MID - HALF_G, FAN], F32, name="looked_mid")
         looked_last = sb.tile([P, G - MID, FAN], F32, name="looked_last")
         nc.vector.tensor_copy(flat(looked_lo[:, 0:OWN, :]), listed(0, OWN))
         nc.scalar.activation(flat(looked_lo[:, OWN:HALF_G, :]), listed(OWN, HALF_G), COPY)
@@ -105,7 +104,7 @@ def tile_attend_viterbistep_kernel(tc, obs, emit_words, emit_scales, cum, step, 
         words_g = sb.tile([P, G], U16, name="words_g", align_bytes=64)
         nc.vector.tensor_copy(words_g[:], words[:].indirect(state_list[:]))
 
-        obs_bf = sb.tile([P, Q, PACK], BF16, name="obs_bf", align_bytes=64)
+        obs_bf = shared.tile([P, Q, PACK], BF16, name="obs_bf", align_bytes=64, offset=2048)
         nc.gpsimd.tensor_scalar(obs_bf[:], obs_sb[:].rearrange("p j q -> p q j"), 1.0, 0.0, mybir.AluOpType.mult, ADD)
 
         cand = sb.tile([P, MID, FAN], F32, name="cand")
@@ -125,7 +124,6 @@ def tile_attend_viterbistep_kernel(tc, obs, emit_words, emit_scales, cum, step, 
 
         nc.vector.tensor_tensor(cand[:, 0:HALF_G, :], looked_lo[:], step_rows(0, HALF_G), ADD)
         nc.vector.tensor_tensor(cand[:, HALF_G:MID, :], looked_mid[:], step_rows(HALF_G, MID), ADD)
-        nc.vector.tensor_reduce(best[:, 0:EARLY], cand[:, 0:EARLY, :], mybir.AxisListType.X, MAX)
 
         obs_codes = sb.tile([P, Q], U32, name="obs_codes", align_bytes=64)
         obs_plane = shared.tile([P, Q], U8, name="obs_plane", align_bytes=64, offset=0)
@@ -142,10 +140,10 @@ def tile_attend_viterbistep_kernel(tc, obs, emit_words, emit_scales, cum, step, 
             stop=True,
         )
 
-        cand_last = shared.tile([P, G - MID, FAN], F32, name="cand_last", offset=Q)
-        first_round(EARLY, MID)
+        cand_last = shared.tile([P, G - MID, FAN], F32, name="cand_last", offset=2048)
+        first_round(0, MID)
         nc.vector.tensor_tensor(cand_last[:], looked_last[:], step_rows(MID, G), ADD)
-        nc.vector.tensor_tensor(best[:, EARLY:MID], pairs[:, 0, EARLY:MID], pairs[:, 1, EARLY:MID], MAX)
+        nc.vector.tensor_tensor(best[:, 0:MID], pairs[:, 0, 0:MID], pairs[:, 1, 0:MID], MAX)
         nc.vector.tensor_reduce(best[:, MID:G], cand_last[:], mybir.AxisListType.X, MAX)
         finish(0, MID, nc.scalar)
         finish(MID, G, nc.sync)

@@ -125,6 +125,8 @@ def tile_attend_viterbistep_kernel(tc, obs, emit_words, emit_scales, cum, step, 
         nc.vector.tensor_tensor(cand[:, 0:HALF_G, :], looked_lo[:], step_rows(0, HALF_G), ADD)
         nc.vector.tensor_tensor(cand[:, HALF_G:MID, :], looked_mid[:], step_rows(HALF_G, MID), ADD)
 
+        first_round(0, HALF_G)
+
         obs_codes = sb.tile([P, Q], U32, name="obs_codes", align_bytes=64)
         obs_plane = shared.tile([P, Q], U8, name="obs_plane", align_bytes=64, offset=0)
         nc.vector.quantize_mx(
@@ -141,7 +143,7 @@ def tile_attend_viterbistep_kernel(tc, obs, emit_words, emit_scales, cum, step, 
         )
 
         cand_last = shared.tile([P, G - MID, FAN], F32, name="cand_last", offset=2048)
-        first_round(0, MID)
+        first_round(HALF_G, MID)
         nc.vector.tensor_tensor(cand_last[:], looked_last[:], step_rows(MID, G), ADD)
         nc.vector.tensor_tensor(best[:, 0:MID], pairs[:, 0, 0:MID], pairs[:, 1, 0:MID], MAX)
         nc.vector.tensor_reduce(best[:, MID:G], cand_last[:], mybir.AxisListType.X, MAX)

@@ -31,6 +31,7 @@ HALF_G = G // HALVES
 
 OWN = 56
 MID = 192
+POOL_Q = 88
 COPY = mybir.ActivationFunctionType.Copy
 ROW = FAN * 4
 
@@ -47,7 +48,7 @@ def tile_attend_viterbistep_kernel(tc, obs, emit_words, emit_scales, cum, step, 
         words = sb.tile([P, T], U16, name="words", align_bytes=64)
         scales = sb.tile([P, T], U8, name="scales", align_bytes=64)
         cum_sb = sb.tile([P, U], F32, name="cum_sb")
-        step_cols = sb.tile([P, HALVES, FAN], F32, name="step_cols")
+        step_cols = shared.tile([P, HALVES, FAN], F32, name="step_cols", offset=3072)
         obs_sb = sb.tile([P, PACK, Q], F32, name="obs_sb")
         ident = sb.tile([P, P], F32, name="ident")
         emit_plane = sb.tile([P, G], U8, name="emit_plane", align_bytes=64)
@@ -95,17 +96,19 @@ def tile_attend_viterbistep_kernel(tc, obs, emit_words, emit_scales, cum, step, 
 
         looked_lo = shared.tile([P, HALF_G, FAN], F32, name="looked_lo", offset=0)
         looked_mid = sb.tile([P, MID - HALF_G, FAN], F32, name="looked_mid")
-        looked_last = sb.tile([P, G - MID, FAN], F32, name="looked_last")
+        looked_last = shared.tile([P, G - MID, FAN], F32, name="looked_last", offset=3072)
         nc.vector.tensor_copy(flat(looked_lo[:, 0:OWN, :]), listed(0, OWN))
         nc.scalar.activation(flat(looked_lo[:, OWN:HALF_G, :]), listed(OWN, HALF_G), COPY)
         nc.scalar.activation(flat(looked_mid[:]), listed(HALF_G, MID), COPY)
+        obs_bf = shared.tile([P, Q, PACK], BF16, name="obs_bf", align_bytes=64, offset=2048)
+        by_column = obs_sb[:].rearrange("p j q -> p q j")
+        nc.gpsimd.tensor_scalar(obs_bf[:, 0:POOL_Q, :], by_column[:, 0:POOL_Q, :], 1.0, 0.0, mybir.AluOpType.mult, ADD)
+        nc.scalar.activation(obs_bf[:, POOL_Q:Q, :], by_column[:, POOL_Q:Q, :], COPY)
         nc.scalar.activation(flat(looked_last[:]), listed(MID, G), COPY)
 
         words_g = sb.tile([P, G], U16, name="words_g", align_bytes=64)
         nc.vector.tensor_copy(words_g[:], words[:].indirect(state_list[:]))
 
-        obs_bf = shared.tile([P, Q, PACK], BF16, name="obs_bf", align_bytes=64, offset=2048)
-        nc.gpsimd.tensor_scalar(obs_bf[:], obs_sb[:].rearrange("p j q -> p q j"), 1.0, 0.0, mybir.AluOpType.mult, ADD)
 
         cand = sb.tile([P, MID, FAN], F32, name="cand")
         pairs = sb.tile([P, 2, MID], F32, name="pairs")

@@ -110,23 +110,31 @@ def tile_attend_viterbistep_kernel(tc, obs, emit_words, emit_scales, cum, step, 
         nc.vector.tensor_copy(words_g[:], words[:].indirect(state_list[:]))
 
 
-        cand = sb.tile([P, MID, FAN], F32, name="cand")
+        cand = sb.tile([P, 2, MID, 2], F32, name="cand")
         pairs = sb.tile([P, 2, MID], F32, name="pairs")
         best = sb.tile([P, G], F32, name="best")
         result = sb.tile([P, G], F32, name="result")
         emission = psum.tile([P, G], F32, name="emission")
 
         def first_round(lo, hi):
-            quads = cand[:, lo:hi, :].rearrange("p n (a b) -> p n a b", a=2)
-            kept = pairs[:, :, lo:hi].rearrange("p b n -> p n b")
-            nc.vector.tensor_tensor(kept, quads[:, :, 0, :], quads[:, :, 1, :], MAX)
+            kept = pairs[:, :, lo:hi].rearrange("p b (m n) -> p m b n", n=2)
+            left, right = [cand[:, a, lo:hi, :].rearrange("p (m n) b -> p m b n", n=2) for a in range(2)]
+            nc.vector.tensor_tensor(kept, left, right, MAX)
 
         def finish(lo, hi, queue):
             nc.vector.tensor_tensor(result[:, lo:hi], best[:, lo:hi], emission[:, lo:hi], ADD)
             queue.dma_start(out[:, lo:hi], result[:, lo:hi])
 
-        nc.vector.tensor_tensor(cand[:, 0:HALF_G, :], looked_lo[:], step_rows(0, HALF_G), ADD)
-        nc.vector.tensor_tensor(cand[:, HALF_G:MID, :], looked_mid[:], step_rows(HALF_G, MID), ADD)
+        def add_step(lo, hi, looked):
+            nc.vector.tensor_tensor(
+                cand[:, :, lo:hi, :].rearrange("p a n b -> p n a b"),
+                looked.rearrange("p n (a b) -> p n a b", a=2),
+                step_rows(lo, hi).rearrange("p n (a b) -> p n a b", a=2),
+                ADD,
+            )
+
+        add_step(0, HALF_G, looked_lo[:])
+        add_step(HALF_G, MID, looked_mid[:])
 
         first_round(0, HALF_G)
 

@@ -50,14 +50,14 @@ def tile_attend_viterbistep_kernel(tc, obs, emit_words, emit_scales, cum, step, 
         cum_sb = sb.tile([P, U], F32, name="cum_sb")
         step_cols = shared.tile([P, HALVES, FAN], F32, name="step_cols", offset=3072)
         obs_sb = sb.tile([P, PACK, Q], F32, name="obs_sb")
-        ident = sb.tile([P, P], F32, name="ident")
+        ident = shared.tile([P, P], F32, name="ident", offset=4096)
         emit_plane = sb.tile([P, G], U8, name="emit_plane", align_bytes=64)
 
         nc.vector.memset(scales[0 : P - BLOCKS, :].bitcast(I32), 0)
         make_identity(nc, ident[:])
         nc.gpsimd.memset(emit_plane[:].bitcast(I32), 0)
 
-        nc.sync.dma_start(step_cols[:], step.rearrange("o (h n r) -> (o n) h r", h=HALVES, r=FAN))
+        nc.sync.dma_start(step_cols[:], step.rearrange("o (n h r) -> (o n) h r", h=HALVES, r=FAN))
         nc.scalar.dma_start(scales[P - BLOCKS : P, :].bitcast(I32), emit_scales[0].bitcast(I32))
         nc.sync.dma_start(state_list[:], offs)
         nc.scalar.dma_start(cum_sb[:], cum)
@@ -76,9 +76,11 @@ def tile_attend_viterbistep_kernel(tc, obs, emit_words, emit_scales, cum, step, 
                 nc.tensor.transpose(bank[:, r, :], step_cols[:, h, r : r + 1].to_broadcast([P, P]), ident[:])
             banks.append(bank)
 
-        def step_rows(lo, hi):
-            h, first = divmod(lo, HALF_G)
-            return banks[h][:, :, first : first + hi - lo].rearrange("p r n -> p n r")
+        def step_rows(lo, hi, parity):
+            return banks[parity][:, :, lo // 2 : hi // 2].rearrange("p r n -> p n r")
+
+        def of_parity(ap, parity):
+            return ap.rearrange("p (n s) r -> p n s r", s=2)[:, :, parity, :]
 
         def listed(lo, hi):
             return cum_sb[:].indirect(pred_list[:, lo * FAN // LIST_COL : hi * FAN // LIST_COL])
@@ -110,33 +112,33 @@ def tile_attend_viterbistep_kernel(tc, obs, emit_words, emit_scales, cum, step, 
         nc.vector.tensor_copy(words_g[:], words[:].indirect(state_list[:]))
 
 
-        cand = sb.tile([P, 2, MID, 2], F32, name="cand")
-        pairs = sb.tile([P, 2, MID], F32, name="pairs")
+        cand_lo = sb.tile([P, 2, HALF_G // 2, FAN], F32, name="cand_lo")
+        cand_mid = shared.tile([P, 2, (MID - HALF_G) // 2, FAN], F32, name="cand_mid", offset=4096)
+        pairs = sb.tile([P, MID, 2], F32, name="pairs")
         best = sb.tile([P, G], F32, name="best")
         result = sb.tile([P, G], F32, name="result")
         emission = psum.tile([P, G], F32, name="emission")
 
-        def first_round(lo, hi):
-            kept = pairs[:, :, lo:hi].rearrange("p b (m n) -> p m b n", n=2)
-            left, right = [cand[:, a, lo:hi, :].rearrange("p (m n) b -> p m b n", n=2) for a in range(2)]
-            nc.vector.tensor_tensor(kept, left, right, MAX)
+        def first_round(lo, hi, cand):
+            left, right = [
+                cand[:, :, :, 2 * a : 2 * a + 2].rearrange("p s n b -> p n s b") for a in range(2)
+            ]
+            nc.vector.tensor_tensor(pairs[:, lo:hi, :].rearrange("p (n s) b -> p n s b", s=2), left, right, MAX)
 
         def finish(lo, hi, queue):
             nc.vector.tensor_tensor(result[:, lo:hi], best[:, lo:hi], emission[:, lo:hi], ADD)
             queue.dma_start(out[:, lo:hi], result[:, lo:hi])
 
-        def add_step(lo, hi, looked):
-            nc.vector.tensor_tensor(
-                cand[:, :, lo:hi, :].rearrange("p a n b -> p n a b"),
-                looked.rearrange("p n (a b) -> p n a b", a=2),
-                step_rows(lo, hi).rearrange("p n (a b) -> p n a b", a=2),
-                ADD,
-            )
+        def add_step(lo, hi, looked, into):
+            for parity in range(2):
+                nc.vector.tensor_tensor(
+                    into[:, parity, :, :], of_parity(looked, parity), step_rows(lo, hi, parity), ADD
+                )
 
-        add_step(0, HALF_G, looked_lo[:])
-        add_step(HALF_G, MID, looked_mid[:])
+        add_step(0, HALF_G, looked_lo[:], cand_lo[:])
+        add_step(HALF_G, MID, looked_mid[:], cand_mid[:])
 
-        first_round(0, HALF_G)
+        first_round(0, HALF_G, cand_lo)
 
         obs_codes = sb.tile([P, Q], U32, name="obs_codes", align_bytes=64)
         obs_plane = shared.tile([P, Q], U8, name="obs_plane", align_bytes=64, offset=0)
@@ -153,10 +155,15 @@ def tile_attend_viterbistep_kernel(tc, obs, emit_words, emit_scales, cum, step, 
             stop=True,
         )
 
-        cand_last = shared.tile([P, G - MID, FAN], F32, name="cand_last", offset=2048)
-        first_round(HALF_G, MID)
-        nc.vector.tensor_tensor(cand_last[:], looked_last[:], step_rows(MID, G), ADD)
-        nc.vector.tensor_tensor(best[:, 0:MID], pairs[:, 0, 0:MID], pairs[:, 1, 0:MID], MAX)
-        nc.vector.tensor_reduce(best[:, MID:G], cand_last[:], mybir.AxisListType.X, MAX)
+        cand_last = shared.tile([P, 2, (G - MID) // 2, FAN], F32, name="cand_last", offset=2048)
+        first_round(HALF_G, MID, cand_mid)
+        add_step(MID, G, looked_last[:], cand_last[:])
+        nc.vector.tensor_tensor(best[:, 0:MID], pairs[:, 0:MID, 0], pairs[:, 0:MID, 1], MAX)
+        nc.vector.tensor_reduce(
+            best[:, MID:G].rearrange("p (n s) -> p n s", s=2),
+            cand_last[:].rearrange("p s n r -> p n s r"),
+            mybir.AxisListType.X,
+            MAX,
+        )
         finish(0, MID, nc.scalar)
         finish(MID, G, nc.sync)

from contextlib import ExitStack

import concourse.mybir as mybir
from concourse.masks import make_identity

D, T, G, U, I, Q = 512, 1024, 256, 1024, 1024, 128
FLOPS = 2 * D * Q * G

F32 = mybir.dt.float32
BF16 = mybir.dt.bfloat16
I32 = mybir.dt.int32
U32 = mybir.dt.uint32
U16 = mybir.dt.uint16
U8 = mybir.dt.uint8
FP8X4 = mybir.dt.float8_e4m3fn_x4
FP4X4 = mybir.dt.float4_e2m1fn_x4
ADD = mybir.AluOpType.add
MAX = mybir.AluOpType.max

P = 128
PACK = 4
BLOCKS = D // 32
QUADRANTS = 4
QUAD_ROWS = BLOCKS // QUADRANTS
LIST_COL = 16
FAN = I // G
HALVES = 2
HALF_I = I // HALVES
HALF_G = G // HALVES


OWN = 56
MID = 192
POOL_Q = 88
COPY = mybir.ActivationFunctionType.Copy
ROW = FAN * 4


def tile_attend_viterbistep_kernel(tc, obs, emit_words, emit_scales, cum, step, offs, offs2, out):
    nc = tc.nc
    with ExitStack() as ctx:
        sb = ctx.enter_context(tc.tile_pool(name="sb", bufs=1))
        shared = ctx.enter_context(tc.tile_pool(name="shared", bufs=1))
        psum = ctx.enter_context(tc.psum_pool(name="psum", bufs=1))

        state_list = sb.tile([P, G // LIST_COL], U16, name="state_list")
        pred_list = sb.tile([P, I // LIST_COL], U16, name="pred_list")
        words = sb.tile([P, T], U16, name="words", align_bytes=64)
        scales = sb.tile([P, T], U8, name="scales", align_bytes=64)
        cum_sb = sb.tile([P, U], F32, name="cum_sb")
        step_cols = shared.tile([P, HALVES, FAN], F32, name="step_cols", offset=3072)
        obs_sb = sb.tile([P, PACK, Q], F32, name="obs_sb")
        ident = shared.tile([P, P], F32, name="ident", offset=4096)
        emit_plane = sb.tile([P, G], U8, name="emit_plane", align_bytes=64)

        nc.vector.memset(scales[0 : P - BLOCKS, :].bitcast(I32), 0)
        make_identity(nc, ident[:])
        nc.gpsimd.memset(emit_plane[:].bitcast(I32), 0)

        nc.sync.dma_start(step_cols[:], step.rearrange("o (n h r) -> (o n) h r", h=HALVES, r=FAN))
        nc.scalar.dma_start(scales[P - BLOCKS : P, :].bitcast(I32), emit_scales[0].bitcast(I32))
        nc.sync.dma_start(state_list[:], offs)
        nc.scalar.dma_start(cum_sb[:], cum)
        nc.sync.dma_start(pred_list[:], offs2)
        nc.sync.dma_start(words[:].bitcast(I32), emit_words[0].bitcast(I32))
        nc.sync.dma_start(obs_sb[:], obs.rearrange("(p j) q -> p j q", j=PACK))

        warm = sb.tile([P, 16], F32, name="warm")
        nc.vector.memset(warm[:, 0:1], 0.0)
        nc.scalar.activation(warm[:, 8:9], warm[:, 0:1], COPY)

        banks = []
        for h in range(HALVES):
            bank = psum.tile([P, FAN, P], F32, name="step_bank%d" % h)
            for r in range(FAN):
                nc.tensor.transpose(bank[:, r, :], step_cols[:, h, r : r + 1].to_broadcast([P, P]), ident[:])
            banks.append(bank)

        def step_rows(lo, hi, parity):
            return banks[parity][:, :, lo // 2 : hi // 2].rearrange("p r n -> p n r")

        def of_parity(ap, parity):
            return ap.rearrange("p (n s) r -> p n s r", s=2)[:, :, parity, :]

        def listed(lo, hi):
            return cum_sb[:].indirect(pred_list[:, lo * FAN // LIST_COL : hi * FAN // LIST_COL])

        def flat(ap):
            return ap.rearrange("p n r -> p (n r)")

        scales_g = sb.tile([P, G], U8, name="scales_g", align_bytes=64)
        nc.vector.tensor_copy(scales_g[:], scales[:].indirect(state_list[:]))
        for quad in range(QUADRANTS):
            nc.sync.dma_start(
                emit_plane[32 * quad : 32 * quad + QUAD_ROWS, :].bitcast(I32),
                scales_g[P - BLOCKS + QUAD_ROWS * quad : P - BLOCKS + QUAD_ROWS * (quad + 1), :].bitcast(I32),
            )

        looked_lo = shared.tile([P, HALF_G, FAN], F32, name="looked_lo", offset=0)
        looked_mid = sb.tile([P, MID - HALF_G, FAN], F32, name="looked_mid")
        looked_last = shared.tile([P, G - MID, FAN], F32, name="looked_last", offset=3072)
        nc.vector.tensor_copy(flat(looked_lo[:, 0:OWN, :]), listed(0, OWN))
        nc.scalar.activation(flat(looked_lo[:, OWN:HALF_G, :]), listed(OWN, HALF_G), COPY)
        nc.scalar.activation(flat(looked_mid[:]), listed(HALF_G, MID), COPY)
        obs_bf = shared.tile([P, Q, PACK], BF16, name="obs_bf", align_bytes=64, offset=2048)
        by_column = obs_sb[:].rearrange("p j q -> p q j")
        nc.gpsimd.tensor_scalar(obs_bf[:, 0:POOL_Q, :], by_column[:, 0:POOL_Q, :], 1.0, 0.0, mybir.AluOpType.mult, ADD)
        nc.scalar.activation(obs_bf[:, POOL_Q:Q, :], by_column[:, POOL_Q:Q, :], COPY)
        nc.scalar.activation(flat(looked_last[:]), listed(MID, G), COPY)

        words_g = sb.tile([P, G], U16, name="words_g", align_bytes=64)
        nc.vector.tensor_copy(words_g[:], words[:].indirect(state_list[:]))


        cand_lo = sb.tile([P, 2, HALF_G // 2, FAN], F32, name="cand_lo")
        cand_mid = shared.tile([P, 2, (MID - HALF_G) // 2, FAN], F32, name="cand_mid", offset=4096)
        pairs = sb.tile([P, MID, 2], F32, name="pairs")
        best = sb.tile([P, G], F32, name="best")
        result = sb.tile([P, G], F32, name="result")
        emission = psum.tile([P, G], F32, name="emission")

        def first_round(lo, hi, cand):
            left, right = [
                cand[:, :, :, 2 * a : 2 * a + 2].rearrange("p s n b -> p n s b") for a in range(2)
            ]
            nc.vector.tensor_tensor(pairs[:, lo:hi, :].rearrange("p (n s) b -> p n s b", s=2), left, right, MAX)

        def finish(lo, hi, queue):
            nc.vector.tensor_tensor(result[:, lo:hi], best[:, lo:hi], emission[:, lo:hi], ADD)
            queue.dma_start(out[:, lo:hi], result[:, lo:hi])

        def add_step(lo, hi, looked, into):
            for parity in range(2):
                nc.vector.tensor_tensor(
                    into[:, parity, :, :], of_parity(looked, parity), step_rows(lo, hi, parity), ADD
                )

        add_step(0, HALF_G, looked_lo[:], cand_lo[:])
        add_step(HALF_G, MID, looked_mid[:], cand_mid[:])

        first_round(0, HALF_G, cand_lo)

        obs_codes = sb.tile([P, Q], U32, name="obs_codes", align_bytes=64)
        obs_plane = shared.tile([P, Q], U8, name="obs_plane", align_bytes=64, offset=0)
        nc.vector.quantize_mx(
            out=obs_codes[:].bitcast(FP8X4), scales=obs_plane[:], in_=obs_bf[:].rearrange("p q j -> p (q j)")
        )
        nc.tensor.matmul_mx(
            out=emission[:],
            lhsT=obs_codes[:].bitcast(FP8X4),
            lhsT_scale=obs_plane[:],
            rhs=words_g[:].bitcast(FP4X4),
            rhs_scale=emit_plane[:],
            start=True,
            stop=True,
        )

        cand_last = shared.tile([P, 2, (G - MID) // 2, FAN], F32, name="cand_last", offset=2048)
        first_round(HALF_G, MID, cand_mid)
        add_step(MID, G, looked_last[:], cand_last[:])
        nc.vector.tensor_tensor(best[:, 0:MID], pairs[:, 0:MID, 0], pairs[:, 0:MID, 1], MAX)
        nc.vector.tensor_reduce(
            best[:, MID:G].rearrange("p (n s) -> p n s", s=2),
            cand_last[:].rearrange("p s n r -> p n s r"),
            mybir.AxisListType.X,
            MAX,
        )
        finish(0, MID, nc.scalar)
        finish(MID, G, nc.sync)
